import numpy as np
import ml_dtypes


def mxq(x, axis, fmt="e4m3"):
    dtype, down = {"e4m3": (ml_dtypes.float8_e4m3fn, 7), "e5m2": (ml_dtypes.float8_e5m2, 14)}[fmt]
    v = np.moveaxis(np.asarray(x, np.float32).astype(ml_dtypes.bfloat16).astype(np.float64), axis, -1)
    blocks = v.reshape(v.shape[:-1] + (-1, 32))
    amax = np.abs(blocks).max(-1, keepdims=True)
    byte = np.maximum(np.where(amax > 0, np.frexp(amax)[1] - 1 + 127, 0) - down, 1)
    scale = np.exp2(byte - 127.0)
    codes = (blocks / scale).astype(np.float32).astype(dtype).astype(np.float64)
    return np.moveaxis((codes * scale).reshape(v.shape), -1, axis)


WIDE = False


def mx_kscale(k):
    if not WIDE:
        return np.ones(k)
    levels = np.array([10, -10, 5, -5, 0])
    if k % 512:
        return np.exp2(np.random.permutation(np.resize(levels, k // 32))).repeat(32)
    a = np.empty((k // 512, 16))
    for p in range(k // 512):
        a[p, :8] = np.random.permutation(np.resize(levels, 8))
        for g in range(8):
            far = levels[np.abs(levels - a[p, g]) >= 10]
            a[p, g + 8] = far[np.random.randint(len(far))]
    return np.exp2(a.ravel()).repeat(32)


BF16 = ml_dtypes.bfloat16


def bf(x):
    return np.asarray(x, np.float32).astype(BF16)


def f64(x):
    return np.asarray(x).astype(np.float64)


E2M1 = np.array([0.0, 0.5, 1.0, 1.5, 2.0, 3.0, 4.0, 6.0, -0.0, -0.5, -1.0, -1.5, -2.0, -3.0, -4.0, -6.0])


def pack_weight(w, fmt):
    k, n = w.shape
    w = f64(bf(w)).reshape(k // 32, 32, n)
    amax = np.abs(w).max(1)
    if fmt == "e4m3":
        byte = np.frexp(amax)[1] - 1 + 127 - 7
    else:
        mant, ex = np.frexp(amax / 6.0)
        byte = np.where(mant > 0.5, ex, ex - 1) + 127
    byte = np.clip(np.where(amax > 0, byte, 1), 1, 254)
    scaled = (w * np.exp2(127.0 - byte)[:, None, :]).reshape(k, n).astype(np.float32)
    by_word = np.ascontiguousarray(scaled.reshape(k // 512, 128, 4, n).transpose(0, 1, 3, 2))
    if fmt == "e4m3":
        words = by_word.astype(ml_dtypes.float8_e4m3fn).view(np.uint8)
    else:
        c = by_word.astype(ml_dtypes.float4_e2m1fn).view(np.uint8) & 0xF
        words = c[..., 0::2] | (c[..., 1::2] << 4)
    return np.ascontiguousarray(words), np.ascontiguousarray(byte.astype(np.uint8).reshape(k // 512, 16, n))


def unpack_weight(words, scales, fmt):
    g, p, n, _ = words.shape
    if fmt == "e4m3":
        vals = np.ascontiguousarray(words).view(ml_dtypes.float8_e4m3fn).astype(np.float64)
    else:
        nib = np.empty((g, p, n, 4), np.uint8)
        nib[..., 0::2] = words & 0xF
        nib[..., 1::2] = words >> 4
        vals = E2M1[nib]
    vals = vals * np.repeat(np.exp2(scales.astype(np.float64) - 127.0), 8, axis=1)[..., None]
    return vals.transpose(0, 1, 3, 2).reshape(g * 512, n)
def pack4(w):
    words, scales = pack_weight(w, "e2m1")
    return words.reshape(words.shape[0], 128, -1), scales


def unpack4(words, scales):
    return unpack_weight(words.reshape(words.shape[0], 128, -1, 2), scales, "e2m1")


Q, T, D, G = 512, 2048, 1024, 1536


def setup_inputs():
    s = mx_kscale(D)
    u = mx_kscale(G)
    t = mx_kscale(D)
    grad = np.random.standard_normal((G, T)) * u[:, None]
    proj = np.random.standard_normal((G, D)) / np.sqrt(G) / u[:, None] / t
    grad_words, grad_scales = pack4(grad)
    proj_words, proj_scales = pack4(proj)
    return {"phi_q": bf(np.random.standard_normal((Q, D)) * s),
            "kinv": bf(0.25 * np.random.standard_normal((D, D)) / np.sqrt(D) / s[:, None] * t),
            "miss_q": bf(np.random.uniform(0.2, 1.0, Q)),
            "grad_words": grad_words, "grad_scales": grad_scales,
            "proj_words": proj_words, "proj_scales": proj_scales,
            "mu": bf(0.4 * np.random.standard_normal(D) / t),
            "miss_t": bf(np.random.uniform(0.2, 1.0, T))}


def reference(phi_q, kinv, miss_q, grad_words, grad_scales, proj_words, proj_scales, mu, miss_t):
    h = mxq(f64(phi_q), 1, "e4m3") @ mxq(f64(kinv), 0, "e4m3")
    h = h * f64(miss_q)[:, None]
    grad = unpack4(grad_words, grad_scales)
    proj = unpack4(proj_words, proj_scales)
    phi = grad.T @ proj
    phi = (phi - f64(mu)) * f64(miss_t)[:, None]
    return mxq(h, 1, "e4m3") @ mxq(phi, 1, "e4m3").T

@@ -1,0 +1,367 @@
+from contextlib import ExitStack
+
+import concourse.mybir as mybir
+from concourse.masks import make_identity
+
+Q, T, D, G = 512, 2048, 1024, 1536
+FLOPS = 2 * (Q * D * D + T * D * G + Q * T * D)
+
+F32 = mybir.dt.float32
+BF16 = mybir.dt.bfloat16
+I32 = mybir.dt.int32
+U32 = mybir.dt.uint32
+U8 = mybir.dt.uint8
+FP8X4 = mybir.dt.float8_e4m3fn_x4
+FP4X4 = mybir.dt.float4_e2m1fn_x4
+ALU = mybir.AluOpType
+
+P = 128
+PACK = 4
+PASS = P * PACK
+GRAD_PASSES = G // PASS
+FEAT_PASSES = D // PASS
+CHUNKS = T // PASS
+BANKS = 8
+
+
+def tile_trak_attribution_scores_s12_kernel(
+    tc, phi_q, kinv, miss_q, grad_words, grad_scales, proj_words, proj_scales, mu, miss_t, out
+):
+    nc = tc.nc
+    with ExitStack() as ctx:
+        keep = ctx.enter_context(tc.tile_pool(name="keep", bufs=1))
+        ring = ctx.enter_context(tc.tile_pool(name="ring", bufs=1))
+        psum = ctx.enter_context(tc.psum_pool(name="psum", bufs=1))
+        ctx.enter_context(tc.manual_schedule())
+
+        def kept(name, shape, dtype):
+            return keep.tile(shape, dtype, name=name, align_bytes=64)
+
+        banks_taken = []
+
+        def next_bank(shape, dtype):
+            name = "bank%d" % (len(banks_taken) % BANKS)
+            banks_taken.append(name)
+            return psum.tile(shape, dtype, name=name, tag=name)
+
+        halves = range(FEAT_PASSES)
+        ident = kept("ident", [P, P], F32)
+        ident_bf = kept("ident_bf", [P, P], BF16)
+        proj_raw = [kept("proj_raw%d" % g, [P, GRAD_PASSES, 2 * PASS], U8) for g in halves]
+        proj = [kept("proj%d" % g, [P, GRAD_PASSES, 2 * PASS], U8) for g in halves]
+        proj_sc_raw = [kept("proj_sc_raw%d" % g, [P, GRAD_PASSES, PASS], U8) for g in halves]
+        proj_sc = [kept("proj_sc%d" % g, [P, GRAD_PASSES, PASS], U8) for g in halves]
+        grad = [kept("grad%d" % c, [P, GRAD_PASSES, 2 * PASS], U8) for c in range(CHUNKS)]
+        grad_sc_first = kept("grad_sc_first", [P, GRAD_PASSES, PASS], U8)
+        grad_sc_rest = kept("grad_sc_rest", [P, GRAD_PASSES, T - PASS], U8)
+        mu_rows = kept("mu_rows", [P, FEAT_PASSES * P], BF16)
+        mu_cols = kept("mu_cols", [P, FEAT_PASSES, PACK], F32)
+        miss_t_rows = kept("miss_t_rows", [P, T // P], BF16)
+        miss_q_rows = kept("miss_q_rows", [P, Q // P], BF16)
+        miss_t_all = kept("miss_t_all", [P, T], BF16)
+        miss_q_all = kept("miss_q_all", [P, Q], BF16)
+        query_raw = kept("query_raw", [P, PACK * D], BF16)
+        query_words = kept("query_words", [P, FEAT_PASSES * Q * PACK], BF16)
+        kinv_raw = {}
+        kinv_words = {}
+        h_words = [kept("h_words%d" % g, [P, Q * PACK], BF16) for g in halves]
+        for k in halves:
+            for g in halves:
+                kinv_raw[k, g] = kept("kinv_raw%d%d" % (k, g), [P, PACK, PASS], BF16)
+                kinv_words[k, g] = kept("kinv_words%d%d" % (k, g), [P, PASS * PACK], BF16)
+        phi_slots = {}
+        phi_words = {}
+        phi_banks = {}
+        h_banks = {}
+        out_banks = {}
+        query_banks = {}
+        mx = {}
+
+        def load_scales(tile, scales, first, width):
+            rows = scales.bitcast(I32)
+            for r in range(4):
+                nc.sync.dma_start(
+                    out=tile[:].bitcast(I32)[r:P:32, :, :],
+                    in_=rows[:, r:16:4, first // 4 : (first + width) // 4].rearrange("k q n -> q k n"),
+                )
+
+        def load_words(tile, words, first):
+            nc.sync.dma_start(
+                out=tile[:].bitcast(I32),
+                in_=words.bitcast(I32)[:, :, first // 2 : (first + PASS) // 2].rearrange("k p n -> p k n"),
+            )
+
+        def load_kinv(k, g):
+            nc.sync.dma_start(
+                out=kinv_raw[k, g][:],
+                in_=kinv[k * PASS : (k + 1) * PASS, g * PASS : (g + 1) * PASS].rearrange("(p j) n -> p j n", j=PACK),
+            )
+
+        def sort_proj_words(g):
+            nc.vector.tensor_copy(
+                out=proj[g][:].bitcast(I32).rearrange("p k (s c w) -> p s k c w", s=PACK, w=2),
+                in_=proj_raw[g][:].bitcast(I32).rearrange("p k (c s w) -> p s k c w", s=PACK, w=2),
+            )
+
+        def sort_proj_scales(g):
+            nc.vector.tensor_copy(
+                out=proj_sc[g][:].bitcast(I32).rearrange("p k (s c) -> p s k c", s=PACK),
+                in_=proj_sc_raw[g][:].bitcast(I32).rearrange("p k (c s) -> p s k c", s=PACK),
+            )
+
+        def spread(rows, first_word, count):
+            bank = next_bank([P, count, P], F32)
+            words = rows[:].bitcast(F32)
+            for u in range(count):
+                w = first_word + u
+                nc.tensor.transpose(bank[:, u, :], words[:, w : w + 1].to_broadcast([P, P]), ident[:])
+            return bank
+
+        def quantise(name, words):
+            codes = kept("codes_" + name, [P, PASS], U32)
+            scales = kept("scales_" + name, [P, PASS], U8)
+            nc.vector.quantize_mx(out=codes[:].bitcast(FP8X4), scales=scales[:], in_=words)
+            mx[name] = (codes, scales)
+
+        def phi_matmul(c, g, s):
+            bank = next_bank([P, PASS], F32)
+            for k in range(GRAD_PASSES):
+                if c == 0:
+                    moving_scales = grad_sc_first[:, k, :]
+                else:
+                    moving_scales = grad_sc_rest[:, k, (c - 1) * PASS : c * PASS]
+                nc.tensor.matmul_mx(
+                    out=bank[:],
+                    lhsT=proj[g][:, k, 2 * P * s : 2 * P * (s + 1)].bitcast(FP4X4),
+                    lhsT_scale=proj_sc[g][:, k, P * s : P * (s + 1)],
+                    rhs=grad[c][:, k, :].bitcast(FP4X4),
+                    rhs_scale=moving_scales,
+                    start=(k == 0),
+                    stop=(k == GRAD_PASSES - 1),
+                )
+            if s == 0:
+                phi_slots[c, g] = kept("phi_slots%d%d" % (c, g), [P, PACK, PASS], BF16)
+            nc.vector.scalar_tensor_tensor(
+                out=phi_slots[c, g][:, s, :],
+                in0=bank[:],
+                scalar=mu_cols[:, g, s : s + 1],
+                in1=miss_t_all[:, c * PASS : (c + 1) * PASS],
+                op0=ALU.subtract,
+                op1=ALU.mult,
+            )
+
+        def interleave_phi(c, g, copy):
+            words = ring.tile([P, PASS * PACK], BF16, name="phi_words", tag="phi_words", bufs=3, align_bytes=64)
+            copy(
+                out=words[:].rearrange("p (n i s) -> p n s i", i=4, s=PACK),
+                in_=phi_slots[c, g][:].rearrange("p s (n i) -> p n s i", i=4),
+            )
+            phi_words[c, g] = words
+
+        def quantise_phi(c, g):
+            quantise("phi%d%d" % (c, g), phi_words[c, g][:])
+
+        def interleave_kinv(k, g, copy):
+            copy(
+                out=kinv_words[k, g][:].rearrange("p (s c i j) -> p c s j i", s=PACK, i=4, j=PACK),
+                in_=kinv_raw[k, g][:].rearrange("p j (c s i) -> p c s j i", s=PACK, i=4),
+            )
+
+        def quantise_kinv(k, g):
+            quantise("kinv%d%d" % (k, g), kinv_words[k, g][:])
+
+        def transpose_queries(a):
+            bank = next_bank([P, FEAT_PASSES, 2, P], F32)
+            words = query_raw[:].bitcast(F32)
+            for k in halves:
+                for u in range(2):
+                    first = a * D // 2 + k * PASS // 2
+                    nc.tensor.transpose(bank[:, k, u, :], words[:, first + u : first + PASS // 2 : 2], ident[:])
+            nc.scalar.copy(
+                out=query_words[:].bitcast(F32).rearrange("p (k a n u) -> p a k n u", k=FEAT_PASSES, a=PACK, u=2)[:, a],
+                in_=bank[:].rearrange("p k u n -> p k n u"),
+            )
+
+        def quantise_queries(k):
+            quantise("query%d" % k, query_words[:, k * Q * PACK : (k + 1) * Q * PACK])
+
+        def h_matmul(g, a):
+            bank = next_bank([P, PACK, P], F32)
+            for s in range(PACK):
+                for k in halves:
+                    w_codes, w_scales = mx["kinv%d%d" % (k, g)]
+                    x_codes, x_scales = mx["query%d" % k]
+                    nc.tensor.matmul_mx(
+                        out=bank[:, s, :],
+                        lhsT=w_codes[:, P * s : P * (s + 1)].bitcast(FP8X4),
+                        lhsT_scale=w_scales[:, P * s : P * (s + 1)],
+                        rhs=x_codes[:, P * a : P * (a + 1)].bitcast(FP8X4),
+                        rhs_scale=x_scales[:, P * a : P * (a + 1)],
+                        start=(k == 0),
+                        stop=(k == FEAT_PASSES - 1),
+                    )
+            factor = miss_q_all[:].rearrange("p (u n e) -> p u n e", u=2, e=2)[:, a // 2, :, a % 2 : a % 2 + 1]
+            nc.vector.tensor_tensor(
+                out=h_words[g][:, a * PASS : (a + 1) * PASS].rearrange("p (n s) -> p n s", s=PACK),
+                in0=bank[:].rearrange("p s n -> p n s"),
+                in1=factor.to_broadcast([P, P, PACK]),
+                op=ALU.mult,
+            )
+
+        def quantise_h(g):
+            quantise("h%d" % g, h_words[g][:])
+
+        def score_matmuls(c, pair):
+            for a in pair:
+                out_banks[c, a] = next_bank([P, PASS], F32)
+            for g in halves:
+                for a in pair:
+                    w_codes, w_scales = mx["h%d" % g]
+                    x_codes, x_scales = mx["phi%d%d" % (c, g)]
+                    nc.tensor.matmul_mx(
+                        out=out_banks[c, a][:],
+                        lhsT=w_codes[:, P * a : P * (a + 1)].bitcast(FP8X4),
+                        lhsT_scale=w_scales[:, P * a : P * (a + 1)],
+                        rhs=x_codes[:].bitcast(FP8X4),
+                        rhs_scale=x_scales[:],
+                        start=(g == 0),
+                        stop=(g == FEAT_PASSES - 1),
+                    )
+
+        def store_scores(c, a, copy):
+            scores = ring.tile([P, PASS], F32, name="scores", tag="scores", bufs=8)
+            copy(out=scores[:], in_=out_banks[c, a][:])
+            nc.sync.dma_start(
+                out=out.rearrange("(p a) t -> p a t", a=PACK)[:, a, c * PASS : (c + 1) * PASS], in_=scores[:]
+            )
+
+        on_s = nc.scalar.copy
+        on_v = nc.vector.tensor_copy
+
+        nc.vector.memset(proj_sc_raw[0][:].bitcast(I32), 0)
+        nc.vector.memset(grad_sc_first[:].bitcast(I32), 0)
+        nc.vector.memset(mu_rows[:], 0.0)
+        nc.vector.memset(proj_sc_raw[1][:].bitcast(I32), 0)
+        nc.vector.memset(grad_sc_rest[:].bitcast(I32), 0)
+        nc.gpsimd.dma_start(out=miss_t_rows[:], in_=miss_t.rearrange("(p e) -> p e", p=P))
+        nc.gpsimd.dma_start(
+            out=mu_rows[0:PACK, :].rearrange("s (c i) -> s c i", i=4),
+            in_=mu.rearrange("(c s i) -> s c i", s=PACK, i=4),
+        )
+        make_identity(nc, ident[:])
+        nc.gpsimd.dma_start(out=miss_q_rows[:], in_=miss_q.rearrange("(p a) -> p a", p=P))
+        nc.scalar.copy(out=ident_bf[:], in_=ident[:])
+
+        load_words(proj_raw[0], proj_words, 0)
+        load_words(grad[0], grad_words, 0)
+        load_scales(proj_sc_raw[0], proj_scales, 0, PASS)
+        load_scales(grad_sc_first, grad_scales, 0, PASS)
+        load_words(proj_raw[1], proj_words, PASS)
+        load_scales(proj_sc_raw[1], proj_scales, PASS, PASS)
+        load_kinv(0, 0)
+        load_kinv(1, 0)
+        nc.sync.dma_start(out=query_raw[:], in_=phi_q.rearrange("(p a) k -> p (a k)", a=PACK))
+        load_scales(grad_sc_rest, grad_scales, PASS, T - PASS)
+        load_words(grad[1], grad_words, PASS)
+        load_kinv(0, 1)
+        load_kinv(1, 1)
+        load_words(grad[2], grad_words, 2 * PASS)
+        load_words(grad[3], grad_words, 3 * PASS)
+
+        sort_proj_words(0)
+        sort_proj_scales(0)
+        miss_t_words = miss_t_all[:].bitcast(F32).rearrange("p (n b u) -> p b n u", b=2, u=4)
+        for b in range(2):
+            spread_bank = spread(miss_t_rows, 4 * b, 4)
+            nc.scalar.copy(out=miss_t_words[:, b], in_=spread_bank[:].rearrange("p u n -> p n u"))
+        mu_bank = next_bank([P, FEAT_PASSES, P], BF16)
+        for g in halves:
+            nc.tensor.transpose(mu_bank[:, g, :], mu_rows[:, g * P : (g + 1) * P], ident_bf[:])
+        nc.scalar.copy(out=mu_cols[:], in_=mu_bank[:, :, 0:PACK])
+
+        phi_matmul(0, 0, 0)
+        sort_proj_words(1)
+        phi_matmul(0, 0, 1)
+        sort_proj_scales(1)
+        phi_matmul(0, 0, 2)
+        phi_matmul(0, 0, 3)
+        interleave_kinv(0, 0, on_s)
+        interleave_kinv(1, 0, on_s)
+        phi_matmul(0, 1, 0)
+        phi_matmul(0, 1, 1)
+        quantise_kinv(0, 0)
+        phi_matmul(0, 1, 2)
+        phi_matmul(0, 1, 3)
+        spread_bank = spread(miss_q_rows, 0, 2)
+        nc.scalar.copy(out=miss_q_all[:].bitcast(F32), in_=spread_bank[:].rearrange("p u n -> p (u n)"))
+        for a in range(PACK):
+            transpose_queries(a)
+        quantise_kinv(1, 0)
+        interleave_kinv(0, 1, on_s)
+        interleave_kinv(1, 1, on_s)
+        phi_matmul(1, 0, 0)
+        quantise_queries(0)
+        phi_matmul(1, 0, 1)
+        quantise_queries(1)
+        phi_matmul(1, 0, 2)
+        phi_matmul(1, 0, 3)
+        quantise_kinv(0, 1)
+        phi_matmul(1, 1, 0)
+        phi_matmul(1, 1, 1)
+        phi_matmul(1, 1, 2)
+        quantise_kinv(1, 1)
+        phi_matmul(1, 1, 3)
+        interleave_phi(0, 0, on_s)
+        interleave_phi(0, 1, on_s)
+        for a in range(PACK):
+            h_matmul(0, a)
+        quantise_phi(0, 0)
+        interleave_phi(1, 0, on_s)
+        phi_matmul(2, 0, 0)
+        quantise_h(0)
+        phi_matmul(2, 0, 1)
+        quantise_phi(0, 1)
+        interleave_phi(1, 1, on_s)
+        phi_matmul(2, 0, 2)
+        phi_matmul(2, 0, 3)
+        for a in range(PACK):
+            h_matmul(1, a)
+        quantise_phi(1, 0)
+        interleave_phi(2, 0, on_s)
+        phi_matmul(2, 1, 0)
+        quantise_h(1)
+        phi_matmul(2, 1, 1)
+        quantise_phi(1, 1)
+        phi_matmul(2, 1, 2)
+        phi_matmul(2, 1, 3)
+        for pair in ((0, 1), (2, 3)):
+            score_matmuls(0, pair)
+            for a in pair:
+                store_scores(0, a, on_s)
+        quantise_phi(2, 0)
+        interleave_phi(2, 1, on_s)
+        phi_matmul(3, 0, 0)
+        phi_matmul(3, 0, 1)
+        phi_matmul(3, 0, 2)
+        quantise_phi(2, 1)
+        phi_matmul(3, 0, 3)
+        for pair in ((0, 1), (2, 3)):
+            score_matmuls(1, pair)
+            for a in pair:
+                store_scores(1, a, on_s)
+        interleave_phi(3, 0, on_s)
+        phi_matmul(3, 1, 0)
+        phi_matmul(3, 1, 1)
+        phi_matmul(3, 1, 2)
+        quantise_phi(3, 0)
+        phi_matmul(3, 1, 3)
+        interleave_phi(3, 1, on_v)
+        quantise_phi(3, 1)
+        for pair in ((0, 1), (2, 3)):
+            score_matmuls(2, pair)
+            for a in pair:
+                store_scores(2, a, on_s)
+        for pair in ((0, 1), (2, 3)):
+            score_matmuls(3, pair)
+            store_scores(3, pair[0], on_v)
+            store_scores(3, pair[1], on_s)

@@ -51,7 +51,8 @@ def tile_trak_attribution_scores_s12_kernel(
         proj = [kept("proj%d" % g, [P, GRAD_PASSES, 2 * PASS], U8) for g in halves]
         proj_sc_raw = [kept("proj_sc_raw%d" % g, [P, GRAD_PASSES, PASS], U8) for g in halves]
         proj_sc = [kept("proj_sc%d" % g, [P, GRAD_PASSES, PASS], U8) for g in halves]
-        grad = [kept("grad%d" % c, [P, GRAD_PASSES, 2 * PASS], U8) for c in range(CHUNKS)]
+        grad = [kept("grad%d" % c, [P, GRAD_PASSES, 2 * PASS], U8) for c in range(2)]
+        grad_late = kept("grad_late", [P, GRAD_PASSES, 4 * PASS], U8)
         grad_sc_first = kept("grad_sc_first", [P, GRAD_PASSES, PASS], U8)
         grad_sc_rest = kept("grad_sc_rest", [P, GRAD_PASSES, T - PASS], U8)
         mu_rows = kept("mu_rows", [P, FEAT_PASSES * P], BF16)
@@ -62,12 +63,12 @@ def tile_trak_attribution_scores_s12_kernel(
         miss_q_all = kept("miss_q_all", [P, Q], BF16)
         query_raw = kept("query_raw", [P, PACK * D], BF16)
         query_words = kept("query_words", [P, FEAT_PASSES * Q * PACK], BF16)
-        kinv_raw = {}
+        kinv_early = [kept("kinv_early%d" % g, [P, PACK, PASS], BF16) for g in halves]
+        kinv_late = kept("kinv_late", [P, PACK, D], BF16)
         kinv_words = {}
         h_words = [kept("h_words%d" % g, [P, Q * PACK], BF16) for g in halves]
         for k in halves:
             for g in halves:
-                kinv_raw[k, g] = kept("kinv_raw%d%d" % (k, g), [P, PACK, PASS], BF16)
                 kinv_words[k, g] = kept("kinv_words%d%d" % (k, g), [P, PASS * PACK], BF16)
         phi_slots = {}
         phi_words = {}
@@ -85,16 +86,16 @@ def tile_trak_attribution_scores_s12_kernel(
                     in_=rows[:, r:16:4, first // 4 : (first + width) // 4].rearrange("k q n -> q k n"),
                 )
 
-        def load_words(tile, words, first):
+        def load_words(tile, words, first, width):
             nc.sync.dma_start(
                 out=tile[:].bitcast(I32),
-                in_=words.bitcast(I32)[:, :, first // 2 : (first + PASS) // 2].rearrange("k p n -> p k n"),
+                in_=words.bitcast(I32)[:, :, first // 2 : (first + width) // 2].rearrange("k p n -> p k n"),
             )
 
-        def load_kinv(k, g):
+        def load_kinv(tile, k, first, width):
             nc.sync.dma_start(
-                out=kinv_raw[k, g][:],
-                in_=kinv[k * PASS : (k + 1) * PASS, g * PASS : (g + 1) * PASS].rearrange("(p j) n -> p j n", j=PACK),
+                out=tile[:],
+                in_=kinv[k * PASS : (k + 1) * PASS, first : first + width].rearrange("(p j) n -> p j n", j=PACK),
             )
 
         def sort_proj_words(g):
@@ -118,53 +119,60 @@ def tile_trak_attribution_scores_s12_kernel(
             return bank
 
         def quantise(name, words):
-            codes = kept("codes_" + name, [P, PASS], U32)
-            scales = kept("scales_" + name, [P, PASS], U8)
+            width = words.shape[1] // PACK
+            codes = kept("codes_" + name, [P, width], U32)
+            scales = kept("scales_" + name, [P, width], U8)
             nc.vector.quantize_mx(out=codes[:].bitcast(FP8X4), scales=scales[:], in_=words)
             mx[name] = (codes, scales)
 
-        def phi_matmul(c, g, s):
-            bank = next_bank([P, PASS], F32)
+        def phi_matmul(c, g, s, first=0, width=PASS):
+            bank = next_bank([P, width], F32)
+            t0 = c * PASS + first
             for k in range(GRAD_PASSES):
                 if c == 0:
-                    moving_scales = grad_sc_first[:, k, :]
+                    moving_scales = grad_sc_first[:, k, t0 : t0 + width]
                 else:
-                    moving_scales = grad_sc_rest[:, k, (c - 1) * PASS : c * PASS]
+                    moving_scales = grad_sc_rest[:, k, t0 - PASS : t0 - PASS + width]
+                if c < 2:
+                    moving = grad[c][:, k, 2 * first : 2 * (first + width)]
+                else:
+                    moving = grad_late[:, k, 2 * (t0 - 2 * PASS) : 2 * (t0 - 2 * PASS + width)]
                 nc.tensor.matmul_mx(
                     out=bank[:],
                     lhsT=proj[g][:, k, 2 * P * s : 2 * P * (s + 1)].bitcast(FP4X4),
                     lhsT_scale=proj_sc[g][:, k, P * s : P * (s + 1)],
-                    rhs=grad[c][:, k, :].bitcast(FP4X4),
+                    rhs=moving.bitcast(FP4X4),
                     rhs_scale=moving_scales,
                     start=(k == 0),
                     stop=(k == GRAD_PASSES - 1),
                 )
             if s == 0:
-                phi_slots[c, g] = kept("phi_slots%d%d" % (c, g), [P, PACK, PASS], BF16)
+                phi_slots[c, g, first] = kept("phi_slots%d%d_%d" % (c, g, first), [P, PACK, width], BF16)
             nc.vector.scalar_tensor_tensor(
-                out=phi_slots[c, g][:, s, :],
+                out=phi_slots[c, g, first][:, s, :],
                 in0=bank[:],
                 scalar=mu_cols[:, g, s : s + 1],
-                in1=miss_t_all[:, c * PASS : (c + 1) * PASS],
+                in1=miss_t_all[:, t0 : t0 + width],
                 op0=ALU.subtract,
                 op1=ALU.mult,
             )
 
-        def interleave_phi(c, g, copy):
-            words = ring.tile([P, PASS * PACK], BF16, name="phi_words", tag="phi_words", bufs=3, align_bytes=64)
+        def interleave_phi(c, g, copy, first=0, width=PASS):
+            words = ring.tile([P, width * PACK], BF16, name="phi_words", tag="phi_words", bufs=4, align_bytes=64)
             copy(
-                out=words[:].rearrange("p (n i s) -> p n s i", i=4, s=PACK),
-                in_=phi_slots[c, g][:].rearrange("p s (n i) -> p n s i", i=4),
+                out=words[:].rearrange("p (n s) -> p n s", s=PACK),
+                in_=phi_slots[c, g, first][:].rearrange("p s n -> p n s"),
             )
-            phi_words[c, g] = words
+            phi_words[c, g, first] = words
 
-        def quantise_phi(c, g):
-            quantise("phi%d%d" % (c, g), phi_words[c, g][:])
+        def quantise_phi(c, g, first=0):
+            quantise("phi%d%d_%d" % (c, g, first), phi_words[c, g, first][:])
 
         def interleave_kinv(k, g, copy):
+            rows = kinv_early[g][:] if k == 0 else kinv_late[:, :, g * PASS : (g + 1) * PASS]
             copy(
-                out=kinv_words[k, g][:].rearrange("p (s c i j) -> p c s j i", s=PACK, i=4, j=PACK),
-                in_=kinv_raw[k, g][:].rearrange("p j (c s i) -> p c s j i", s=PACK, i=4),
+                out=kinv_words[k, g][:].rearrange("p (s c i j) -> p c s i j", s=PACK, i=4, j=PACK),
+                in_=rows.rearrange("p j (c s i) -> p c s i j", s=PACK, i=4),
             )
 
         def quantise_kinv(k, g):
@@ -211,62 +219,67 @@ def tile_trak_attribution_scores_s12_kernel(
         def quantise_h(g):
             quantise("h%d" % g, h_words[g][:])
 
-        def score_matmuls(c, pair):
-            for a in pair:
-                out_banks[c, a] = next_bank([P, PASS], F32)
-            for g in halves:
-                for a in pair:
-                    w_codes, w_scales = mx["h%d" % g]
-                    x_codes, x_scales = mx["phi%d%d" % (c, g)]
-                    nc.tensor.matmul_mx(
-                        out=out_banks[c, a][:],
-                        lhsT=w_codes[:, P * a : P * (a + 1)].bitcast(FP8X4),
-                        lhsT_scale=w_scales[:, P * a : P * (a + 1)],
-                        rhs=x_codes[:].bitcast(FP8X4),
-                        rhs_scale=x_scales[:],
-                        start=(g == 0),
-                        stop=(g == FEAT_PASSES - 1),
-                    )
-
-        def store_scores(c, a, copy):
-            scores = ring.tile([P, PASS], F32, name="scores", tag="scores", bufs=8)
-            copy(out=scores[:], in_=out_banks[c, a][:])
-            nc.sync.dma_start(
-                out=out.rearrange("(p a) t -> p a t", a=PACK)[:, a, c * PASS : (c + 1) * PASS], in_=scores[:]
+        def score_pass(c, a, g, first=0, width=PASS):
+            if g == 0:
+                out_banks[c, a, first] = next_bank([P, width], F32)
+            w_codes, w_scales = mx["h%d" % g]
+            if (c, g, first) in phi_words and phi_words[c, g, first].shape[1] == width * PACK:
+                x_codes, x_scales = mx["phi%d%d_%d" % (c, g, first)]
+                columns = slice(0, width)
+            else:
+                x_codes, x_scales = mx["phi%d%d_0" % (c, g)]
+                columns = slice(first, first + width)
+            nc.tensor.matmul_mx(
+                out=out_banks[c, a, first][:],
+                lhsT=w_codes[:, P * a : P * (a + 1)].bitcast(FP8X4),
+                lhsT_scale=w_scales[:, P * a : P * (a + 1)],
+                rhs=x_codes[:, columns].bitcast(FP8X4),
+                rhs_scale=x_scales[:, columns],
+                start=(g == 0),
+                stop=(g == FEAT_PASSES - 1),
             )
+
+        def store_scores(c, a, copy, first=0, width=PASS):
+            scores = ring.tile([P, width], F32, name="scores", tag="scores", bufs=8)
+            copy(out=scores[:], in_=out_banks[c, a, first][:])
+            t0 = c * PASS + first
+            nc.sync.dma_start(out=out.rearrange("(p a) t -> p a t", a=PACK)[:, a, t0 : t0 + width], in_=scores[:])
+
+        def scores_of(c, tiles, copy):
+            for a in tiles:
+                for g in halves:
+                    score_pass(c, a, g)
+                store_scores(c, a, copy)
 
         on_s = nc.scalar.copy
         on_v = nc.vector.tensor_copy
 
         nc.vector.memset(proj_sc_raw[0][:].bitcast(I32), 0)
-        nc.vector.memset(grad_sc_first[:].bitcast(I32), 0)
         nc.vector.memset(mu_rows[:], 0.0)
+        nc.vector.memset(grad_sc_first[:].bitcast(I32), 0)
         nc.vector.memset(proj_sc_raw[1][:].bitcast(I32), 0)
         nc.vector.memset(grad_sc_rest[:].bitcast(I32), 0)
-        nc.gpsimd.dma_start(out=miss_t_rows[:], in_=miss_t.rearrange("(p e) -> p e", p=P))
-        nc.gpsimd.dma_start(
+        make_identity(nc, ident[:])
+        nc.scalar.dma_start(out=miss_t_rows[:], in_=miss_t.rearrange("(p e) -> p e", p=P))
+        load_words(proj_raw[0], proj_words, 0, PASS)
+        nc.scalar.dma_start(
             out=mu_rows[0:PACK, :].rearrange("s (c i) -> s c i", i=4),
             in_=mu.rearrange("(c s i) -> s c i", s=PACK, i=4),
         )
-        make_identity(nc, ident[:])
-        nc.gpsimd.dma_start(out=miss_q_rows[:], in_=miss_q.rearrange("(p a) -> p a", p=P))
         nc.scalar.copy(out=ident_bf[:], in_=ident[:])
-
-        load_words(proj_raw[0], proj_words, 0)
-        load_words(grad[0], grad_words, 0)
         load_scales(proj_sc_raw[0], proj_scales, 0, PASS)
+        load_words(grad[0], grad_words, 0, PASS)
         load_scales(grad_sc_first, grad_scales, 0, PASS)
-        load_words(proj_raw[1], proj_words, PASS)
+        load_kinv(kinv_early[0], 0, 0, PASS)
+        load_words(proj_raw[1], proj_words, PASS, PASS)
         load_scales(proj_sc_raw[1], proj_scales, PASS, PASS)
-        load_kinv(0, 0)
-        load_kinv(1, 0)
+        load_kinv(kinv_early[1], 0, PASS, PASS)
+        nc.sync.dma_start(out=miss_q_rows[:], in_=miss_q.rearrange("(p a) -> p a", p=P))
         nc.sync.dma_start(out=query_raw[:], in_=phi_q.rearrange("(p a) k -> p (a k)", a=PACK))
         load_scales(grad_sc_rest, grad_scales, PASS, T - PASS)
-        load_words(grad[1], grad_words, PASS)
-        load_kinv(0, 1)
-        load_kinv(1, 1)
-        load_words(grad[2], grad_words, 2 * PASS)
-        load_words(grad[3], grad_words, 3 * PASS)
+        load_words(grad[1], grad_words, PASS, PASS)
+        load_kinv(kinv_late, 1, 0, D)
+        load_words(grad_late, grad_words, 2 * PASS, 2 * PASS)
 
         sort_proj_words(0)
         sort_proj_scales(0)
@@ -279,25 +292,27 @@ def tile_trak_attribution_scores_s12_kernel(
             nc.tensor.transpose(mu_bank[:, g, :], mu_rows[:, g * P : (g + 1) * P], ident_bf[:])
         nc.scalar.copy(out=mu_cols[:], in_=mu_bank[:, :, 0:PACK])
 
+        interleave_kinv(0, 0, on_s)
+        interleave_kinv(0, 1, on_s)
         phi_matmul(0, 0, 0)
         sort_proj_words(1)
         phi_matmul(0, 0, 1)
         sort_proj_scales(1)
         phi_matmul(0, 0, 2)
         phi_matmul(0, 0, 3)
-        interleave_kinv(0, 0, on_s)
-        interleave_kinv(1, 0, on_s)
+        interleave_phi(0, 0, on_s)
         phi_matmul(0, 1, 0)
-        phi_matmul(0, 1, 1)
         quantise_kinv(0, 0)
+        phi_matmul(0, 1, 1)
         phi_matmul(0, 1, 2)
+        quantise_kinv(0, 1)
         phi_matmul(0, 1, 3)
         spread_bank = spread(miss_q_rows, 0, 2)
         nc.scalar.copy(out=miss_q_all[:].bitcast(F32), in_=spread_bank[:].rearrange("p u n -> p (u n)"))
         for a in range(PACK):
             transpose_queries(a)
-        quantise_kinv(1, 0)
-        interleave_kinv(0, 1, on_s)
+        quantise_phi(0, 0)
+        interleave_kinv(1, 0, on_s)
         interleave_kinv(1, 1, on_s)
         phi_matmul(1, 0, 0)
         quantise_queries(0)
@@ -305,63 +320,62 @@ def tile_trak_attribution_scores_s12_kernel(
         quantise_queries(1)
         phi_matmul(1, 0, 2)
         phi_matmul(1, 0, 3)
-        quantise_kinv(0, 1)
+        quantise_kinv(1, 0)
         phi_matmul(1, 1, 0)
         phi_matmul(1, 1, 1)
         phi_matmul(1, 1, 2)
         quantise_kinv(1, 1)
         phi_matmul(1, 1, 3)
-        interleave_phi(0, 0, on_s)
         interleave_phi(0, 1, on_s)
+        interleave_phi(1, 0, on_s)
         for a in range(PACK):
             h_matmul(0, a)
-        quantise_phi(0, 0)
-        interleave_phi(1, 0, on_s)
+        quantise_phi(0, 1)
+        interleave_phi(1, 1, on_s)
         phi_matmul(2, 0, 0)
         quantise_h(0)
         phi_matmul(2, 0, 1)
-        quantise_phi(0, 1)
-        interleave_phi(1, 1, on_s)
         phi_matmul(2, 0, 2)
         phi_matmul(2, 0, 3)
+        interleave_phi(2, 0, on_s)
         for a in range(PACK):
             h_matmul(1, a)
-        quantise_phi(1, 0)
-        interleave_phi(2, 0, on_s)
         phi_matmul(2, 1, 0)
         quantise_h(1)
         phi_matmul(2, 1, 1)
-        quantise_phi(1, 1)
         phi_matmul(2, 1, 2)
         phi_matmul(2, 1, 3)
-        for pair in ((0, 1), (2, 3)):
-            score_matmuls(0, pair)
-            for a in pair:
-                store_scores(0, a, on_s)
-        quantise_phi(2, 0)
+        scores_of(0, range(PACK), on_s)
+        quantise_phi(1, 0)
+        quantise_phi(1, 1)
         interleave_phi(2, 1, on_s)
         phi_matmul(3, 0, 0)
+        quantise_phi(2, 0)
         phi_matmul(3, 0, 1)
         phi_matmul(3, 0, 2)
         quantise_phi(2, 1)
         phi_matmul(3, 0, 3)
-        for pair in ((0, 1), (2, 3)):
-            score_matmuls(1, pair)
-            for a in pair:
-                store_scores(1, a, on_s)
+        scores_of(1, (0,), on_s)
         interleave_phi(3, 0, on_s)
-        phi_matmul(3, 1, 0)
-        phi_matmul(3, 1, 1)
-        phi_matmul(3, 1, 2)
+        scores_of(1, (1, 2), on_v)
+        scores_of(1, (3,), on_s)
+        HALF = PASS // 2
+        for s in range(PACK):
+            phi_matmul(3, 1, s, 0, HALF)
         quantise_phi(3, 0)
-        phi_matmul(3, 1, 3)
-        interleave_phi(3, 1, on_v)
-        quantise_phi(3, 1)
-        for pair in ((0, 1), (2, 3)):
-            score_matmuls(2, pair)
-            for a in pair:
-                store_scores(2, a, on_s)
-        for pair in ((0, 1), (2, 3)):
-            score_matmuls(3, pair)
-            store_scores(3, pair[0], on_v)
-            store_scores(3, pair[1], on_s)
+        interleave_phi(3, 1, on_v, 0, HALF)
+        scores_of(2, (0, 1, 2), on_s)
+        quantise_phi(3, 1, 0)
+        for s in range(PACK):
+            phi_matmul(3, 1, s, HALF, HALF)
+        interleave_phi(3, 1, on_v, HALF, HALF)
+        quantise_phi(3, 1, HALF)
+        scores_of(2, (3,), on_s)
+        for a in range(PACK):
+            for g in halves:
+                score_pass(3, a, g, 0, HALF)
+            store_scores(3, a, on_v if a == 2 else on_s, 0, HALF)
+        for a in range(PACK):
+            for g in halves:
+                score_pass(3, a, g, HALF, HALF)
+            store_scores(3, a, on_v if a % 2 == 0 else on_s, HALF, HALF)

@@ -46,7 +46,6 @@ def tile_trak_attribution_scores_s12_kernel(
 
         halves = range(FEAT_PASSES)
         ident = kept("ident", [P, P], F32)
-        ident_bf = kept("ident_bf", [P, P], BF16)
         proj_raw = [kept("proj_raw%d" % g, [P, GRAD_PASSES, 2 * PASS], U8) for g in halves]
         proj = [kept("proj%d" % g, [P, GRAD_PASSES, 2 * PASS], U8) for g in halves]
         proj_sc_raw = [kept("proj_sc_raw%d" % g, [P, GRAD_PASSES, PASS], U8) for g in halves]
@@ -55,8 +54,9 @@ def tile_trak_attribution_scores_s12_kernel(
         grad_late = kept("grad_late", [P, GRAD_PASSES, 4 * PASS], U8)
         grad_sc_first = kept("grad_sc_first", [P, GRAD_PASSES, PASS], U8)
         grad_sc_rest = kept("grad_sc_rest", [P, GRAD_PASSES, T - PASS], U8)
-        mu_rows = kept("mu_rows", [P, FEAT_PASSES * P], BF16)
-        mu_cols = kept("mu_cols", [P, FEAT_PASSES, PACK], F32)
+        mu_raw = kept("mu_raw", [FEAT_PASSES, PASS], BF16)
+        mu_rows = kept("mu_rows", [P, PASS], BF16)
+        mu_cols = kept("mu_cols", [P, 2, FEAT_PASSES, 2], BF16)
         miss_t_rows = kept("miss_t_rows", [P, T // P], BF16)
         miss_q_rows = kept("miss_q_rows", [P, Q // P], BF16)
         miss_t_all = kept("miss_t_all", [P, T], BF16)
@@ -151,7 +151,7 @@ def tile_trak_attribution_scores_s12_kernel(
             nc.vector.scalar_tensor_tensor(
                 out=phi_slots[c, g, first][:, s, :],
                 in0=bank[:],
-                scalar=mu_cols[:, g, s : s + 1],
+                scalar=mu_cols[:, s // 2, g, s % 2 : s % 2 + 1],
                 in1=miss_t_all[:, t0 : t0 + width],
                 op0=ALU.subtract,
                 op1=ALU.mult,
@@ -240,7 +240,7 @@ def tile_trak_attribution_scores_s12_kernel(
             )
 
         def store_scores(c, a, copy, first=0, width=PASS):
-            scores = ring.tile([P, width], F32, name="scores", tag="scores", bufs=8)
+            scores = ring.tile([P, width], F32, name="scores", tag="scores", bufs=14)
             copy(out=scores[:], in_=out_banks[c, a, first][:])
             t0 = c * PASS + first
             nc.sync.dma_start(out=out.rearrange("(p a) t -> p a t", a=PACK)[:, a, t0 : t0 + width], in_=scores[:])
@@ -255,49 +255,50 @@ def tile_trak_attribution_scores_s12_kernel(
         on_v = nc.vector.tensor_copy
 
         nc.vector.memset(proj_sc_raw[0][:].bitcast(I32), 0)
-        nc.vector.memset(mu_rows[:], 0.0)
         nc.vector.memset(grad_sc_first[:].bitcast(I32), 0)
         nc.vector.memset(proj_sc_raw[1][:].bitcast(I32), 0)
+        nc.vector.memset(mu_rows[:], 0.0)
         nc.vector.memset(grad_sc_rest[:].bitcast(I32), 0)
         make_identity(nc, ident[:])
         nc.scalar.dma_start(out=miss_t_rows[:], in_=miss_t.rearrange("(p e) -> p e", p=P))
         load_words(proj_raw[0], proj_words, 0, PASS)
-        nc.scalar.dma_start(
-            out=mu_rows[0:PACK, :].rearrange("s (c i) -> s c i", i=4),
-            in_=mu.rearrange("(c s i) -> s c i", s=PACK, i=4),
-        )
-        nc.scalar.copy(out=ident_bf[:], in_=ident[:])
+        nc.scalar.dma_start(out=mu_raw[:], in_=mu.rearrange("(g d) -> g d", g=FEAT_PASSES))
         load_scales(proj_sc_raw[0], proj_scales, 0, PASS)
         load_words(grad[0], grad_words, 0, PASS)
         load_scales(grad_sc_first, grad_scales, 0, PASS)
-        load_kinv(kinv_early[0], 0, 0, PASS)
-        load_words(proj_raw[1], proj_words, PASS, PASS)
         load_scales(proj_sc_raw[1], proj_scales, PASS, PASS)
+        load_words(proj_raw[1], proj_words, PASS, PASS)
+        load_kinv(kinv_early[0], 0, 0, PASS)
+        load_scales(grad_sc_rest, grad_scales, PASS, T - PASS)
+        load_words(grad[1], grad_words, PASS, PASS)
         load_kinv(kinv_early[1], 0, PASS, PASS)
         nc.sync.dma_start(out=miss_q_rows[:], in_=miss_q.rearrange("(p a) -> p a", p=P))
         nc.sync.dma_start(out=query_raw[:], in_=phi_q.rearrange("(p a) k -> p (a k)", a=PACK))
-        load_scales(grad_sc_rest, grad_scales, PASS, T - PASS)
-        load_words(grad[1], grad_words, PASS, PASS)
         load_kinv(kinv_late, 1, 0, D)
         load_words(grad_late, grad_words, 2 * PASS, 2 * PASS)
 
         sort_proj_words(0)
         sort_proj_scales(0)
+        nc.scalar.copy(
+            out=mu_rows[0:FEAT_PASSES, :].rearrange("g (u c i e) -> g u c i e", u=2, i=4, e=2),
+            in_=mu_raw[:].rearrange("g (c u e i) -> g u c i e", u=2, i=4, e=2),
+        )
         miss_t_words = miss_t_all[:].bitcast(F32).rearrange("p (n b u) -> p b n u", b=2, u=4)
         for b in range(2):
             spread_bank = spread(miss_t_rows, 4 * b, 4)
             nc.scalar.copy(out=miss_t_words[:, b], in_=spread_bank[:].rearrange("p u n -> p n u"))
-        mu_bank = next_bank([P, FEAT_PASSES, P], BF16)
-        for g in halves:
-            nc.tensor.transpose(mu_bank[:, g, :], mu_rows[:, g * P : (g + 1) * P], ident_bf[:])
-        nc.scalar.copy(out=mu_cols[:], in_=mu_bank[:, :, 0:PACK])
+        mu_bank = next_bank([P, 2, P], F32)
+        for u in range(2):
+            nc.tensor.transpose(mu_bank[:, u, :], mu_rows[:].bitcast(F32)[:, u * P : (u + 1) * P], ident[:])
+        nc.scalar.copy(
+            out=mu_cols[:].rearrange("p u g e -> p u (g e)").bitcast(F32), in_=mu_bank[:, :, 0:FEAT_PASSES]
+        )
 
         interleave_kinv(0, 0, on_s)
-        interleave_kinv(0, 1, on_s)
-        phi_matmul(0, 0, 0)
-        sort_proj_words(1)
-        phi_matmul(0, 0, 1)
         sort_proj_scales(1)
+        sort_proj_words(1)
+        phi_matmul(0, 0, 0)
+        phi_matmul(0, 0, 1)
         phi_matmul(0, 0, 2)
         phi_matmul(0, 0, 3)
         interleave_phi(0, 0, on_s)
@@ -305,40 +306,44 @@ def tile_trak_attribution_scores_s12_kernel(
         quantise_kinv(0, 0)
         phi_matmul(0, 1, 1)
         phi_matmul(0, 1, 2)
-        quantise_kinv(0, 1)
         phi_matmul(0, 1, 3)
+        interleave_kinv(0, 1, on_v)
+        quantise_phi(0, 0)
+        interleave_phi(0, 1, on_s)
+        phi_matmul(1, 0, 0)
+        phi_matmul(1, 0, 1)
+        phi_matmul(1, 0, 2)
+        quantise_kinv(0, 1)
+        phi_matmul(1, 0, 3)
+        interleave_kinv(1, 0, on_s)
         spread_bank = spread(miss_q_rows, 0, 2)
         nc.scalar.copy(out=miss_q_all[:].bitcast(F32), in_=spread_bank[:].rearrange("p u n -> p (u n)"))
-        for a in range(PACK):
-            transpose_queries(a)
-        quantise_phi(0, 0)
-        interleave_kinv(1, 0, on_s)
-        interleave_kinv(1, 1, on_s)
-        phi_matmul(1, 0, 0)
-        quantise_queries(0)
-        phi_matmul(1, 0, 1)
-        quantise_queries(1)
-        phi_matmul(1, 0, 2)
-        phi_matmul(1, 0, 3)
-        quantise_kinv(1, 0)
+        transpose_queries(0)
+        transpose_queries(1)
+        quantise_phi(0, 1)
         phi_matmul(1, 1, 0)
         phi_matmul(1, 1, 1)
+        quantise_kinv(1, 0)
+        transpose_queries(2)
+        transpose_queries(3)
+        interleave_kinv(1, 1, on_s)
         phi_matmul(1, 1, 2)
-        quantise_kinv(1, 1)
+        quantise_queries(0)
         phi_matmul(1, 1, 3)
-        interleave_phi(0, 1, on_s)
-        interleave_phi(1, 0, on_s)
-        for a in range(PACK):
-            h_matmul(0, a)
-        quantise_phi(0, 1)
-        interleave_phi(1, 1, on_s)
+        quantise_queries(1)
         phi_matmul(2, 0, 0)
-        quantise_h(0)
         phi_matmul(2, 0, 1)
         phi_matmul(2, 0, 2)
+        quantise_kinv(1, 1)
         phi_matmul(2, 0, 3)
+        interleave_phi(1, 0, on_s)
+        interleave_phi(1, 1, on_s)
         interleave_phi(2, 0, on_s)
         for a in range(PACK):
+            h_matmul(0, a)
+        h_matmul(1, 0)
+        quantise_h(0)
+        for a in range(1, PACK):
             h_matmul(1, a)
         phi_matmul(2, 1, 0)
         quantise_h(1)

@@ -16,12 +16,19 @@ FP4X4 = mybir.dt.float4_e2m1fn_x4
 ALU = mybir.AluOpType
 
 P = 128
-PACK = 4
-PASS = P * PACK
+SLOTS = 4
+PASS = P * SLOTS
+RUN = 4
+QUADRANT = 32
+SCALE_ROWS = 4
 GRAD_PASSES = G // PASS
-FEAT_PASSES = D // PASS
-CHUNKS = T // PASS
+HALVES = D // PASS
+CHUNK = 512
+PIECE = CHUNK // 2
+QUERY_TILES = Q // P
 BANKS = 8
+PHI_WORD_BUFFERS = 4
+SCORE_BUFFERS = 14
 
 
 def tile_trak_attribution_scores_s12_kernel(
@@ -39,51 +46,48 @@ def tile_trak_attribution_scores_s12_kernel(
 
         banks_taken = []
 
-        def next_bank(shape, dtype):
+        def next_bank(shape):
             name = "bank%d" % (len(banks_taken) % BANKS)
             banks_taken.append(name)
-            return psum.tile(shape, dtype, name=name, tag=name)
+            return psum.tile(shape, F32, name=name, tag=name)
 
-        halves = range(FEAT_PASSES)
+        halves = range(HALVES)
         ident = kept("ident", [P, P], F32)
-        proj_raw = [kept("proj_raw%d" % g, [P, GRAD_PASSES, 2 * PASS], U8) for g in halves]
-        proj = [kept("proj%d" % g, [P, GRAD_PASSES, 2 * PASS], U8) for g in halves]
-        proj_sc_raw = [kept("proj_sc_raw%d" % g, [P, GRAD_PASSES, PASS], U8) for g in halves]
-        proj_sc = [kept("proj_sc%d" % g, [P, GRAD_PASSES, PASS], U8) for g in halves]
-        grad = [kept("grad%d" % c, [P, GRAD_PASSES, 2 * PASS], U8) for c in range(2)]
-        grad_late = kept("grad_late", [P, GRAD_PASSES, 4 * PASS], U8)
-        grad_sc_first = kept("grad_sc_first", [P, GRAD_PASSES, PASS], U8)
-        grad_sc_rest = kept("grad_sc_rest", [P, GRAD_PASSES, T - PASS], U8)
-        mu_raw = kept("mu_raw", [FEAT_PASSES, PASS], BF16)
+        proj_raw = [kept("proj_raw%d" % half, [P, GRAD_PASSES, 2 * PASS], U8) for half in halves]
+        proj = [kept("proj%d" % half, [P, GRAD_PASSES, 2 * PASS], U8) for half in halves]
+        proj_sc_raw = [kept("proj_sc_raw%d" % half, [P, GRAD_PASSES, PASS], U8) for half in halves]
+        proj_sc = [kept("proj_sc%d" % half, [P, GRAD_PASSES, PASS], U8) for half in halves]
+        grad_early = [kept("grad%d" % chunk, [P, GRAD_PASSES, 2 * CHUNK], U8) for chunk in range(2)]
+        grad_late = kept("grad_late", [P, GRAD_PASSES, 2 * (T - 2 * CHUNK)], U8)
+        grad_sc_first = kept("grad_sc_first", [P, GRAD_PASSES, CHUNK], U8)
+        grad_sc_rest = kept("grad_sc_rest", [P, GRAD_PASSES, T - CHUNK], U8)
+        mu_raw = kept("mu_raw", [HALVES, PASS], BF16)
         mu_rows = kept("mu_rows", [P, PASS], BF16)
-        mu_cols = kept("mu_cols", [P, 2, FEAT_PASSES, 2], BF16)
+        mu_cols = kept("mu_cols", [P, SLOTS // 2, HALVES, 2], BF16)
         miss_t_rows = kept("miss_t_rows", [P, T // P], BF16)
-        miss_q_rows = kept("miss_q_rows", [P, Q // P], BF16)
+        miss_q_rows = kept("miss_q_rows", [P, QUERY_TILES], BF16)
         miss_t_all = kept("miss_t_all", [P, T], BF16)
         miss_q_all = kept("miss_q_all", [P, Q], BF16)
-        query_raw = kept("query_raw", [P, PACK * D], BF16)
-        query_words = kept("query_words", [P, FEAT_PASSES * Q * PACK], BF16)
-        kinv_early = [kept("kinv_early%d" % g, [P, PACK, PASS], BF16) for g in halves]
-        kinv_late = kept("kinv_late", [P, PACK, D], BF16)
+        query_raw = kept("query_raw", [P, QUERY_TILES * D], BF16)
+        query_sorted = [kept("query_sorted%d" % pair, [P, 2 * D], BF16) for pair in range(QUERY_TILES // 2)]
+        query_words = kept("query_words", [P, HALVES * Q * SLOTS], BF16)
+        kinv_early = [kept("kinv_early%d" % half, [P, SLOTS, PASS], BF16) for half in halves]
+        kinv_late = kept("kinv_late", [P, SLOTS, D], BF16)
+        h_words = [kept("h_words%d" % half, [P, Q * SLOTS], BF16) for half in halves]
         kinv_words = {}
-        h_words = [kept("h_words%d" % g, [P, Q * PACK], BF16) for g in halves]
         for k in halves:
-            for g in halves:
-                kinv_words[k, g] = kept("kinv_words%d%d" % (k, g), [P, PASS * PACK], BF16)
+            for half in halves:
+                kinv_words[k, half] = kept("kinv_words%d%d" % (k, half), [P, PASS * SLOTS], BF16)
         phi_slots = {}
         phi_words = {}
-        phi_banks = {}
-        h_banks = {}
-        out_banks = {}
-        query_banks = {}
-        mx = {}
+        quantised = {}
 
         def load_scales(tile, scales, first, width):
             rows = scales.bitcast(I32)
-            for r in range(4):
+            for r in range(SCALE_ROWS):
                 nc.sync.dma_start(
-                    out=tile[:].bitcast(I32)[r:P:32, :, :],
-                    in_=rows[:, r:16:4, first // 4 : (first + width) // 4].rearrange("k q n -> q k n"),
+                    out=tile[:].bitcast(I32)[r:P:QUADRANT, :, :],
+                    in_=rows[:, r :: SCALE_ROWS, first // 4 : (first + width) // 4].rearrange("k q n -> q k n"),
                 )
 
         def load_words(tile, words, first, width):
@@ -93,294 +97,310 @@ def tile_trak_attribution_scores_s12_kernel(
             )
 
         def load_kinv(tile, k, first, width):
-            nc.sync.dma_start(
-                out=tile[:],
-                in_=kinv[k * PASS : (k + 1) * PASS, first : first + width].rearrange("(p j) n -> p j n", j=PACK),
-            )
+            rows = kinv[k * PASS : (k + 1) * PASS, first : first + width]
+            nc.sync.dma_start(out=tile[:], in_=rows.rearrange("(p j) n -> p j n", j=SLOTS))
 
-        def sort_proj_words(g):
+        def sort_proj_words(half):
             nc.vector.tensor_copy(
-                out=proj[g][:].bitcast(I32).rearrange("p k (s c w) -> p s k c w", s=PACK, w=2),
-                in_=proj_raw[g][:].bitcast(I32).rearrange("p k (c s w) -> p s k c w", s=PACK, w=2),
+                out=proj[half][:].bitcast(I32).rearrange("p k (s c w) -> p s k c w", s=SLOTS, w=2),
+                in_=proj_raw[half][:].bitcast(I32).rearrange("p k (c s w) -> p s k c w", s=SLOTS, w=2),
             )
 
-        def sort_proj_scales(g):
+        def sort_proj_scales(half, partitions):
             nc.vector.tensor_copy(
-                out=proj_sc[g][:].bitcast(I32).rearrange("p k (s c) -> p s k c", s=PACK),
-                in_=proj_sc_raw[g][:].bitcast(I32).rearrange("p k (c s) -> p s k c", s=PACK),
+                out=proj_sc[half][partitions].bitcast(I32).rearrange("p k (s c) -> p s k c", s=SLOTS),
+                in_=proj_sc_raw[half][partitions].bitcast(I32).rearrange("p k (c s) -> p s k c", s=SLOTS),
             )
 
-        def spread(rows, first_word, count):
-            bank = next_bank([P, count, P], F32)
-            words = rows[:].bitcast(F32)
+        def spread(rows, first_pair, count):
+            bank = next_bank([P, count, P])
+            pairs = rows[:].bitcast(F32)
             for u in range(count):
-                w = first_word + u
-                nc.tensor.transpose(bank[:, u, :], words[:, w : w + 1].to_broadcast([P, P]), ident[:])
+                column = pairs[:, first_pair + u : first_pair + u + 1]
+                nc.tensor.transpose(bank[:, u, :], column.to_broadcast([P, P]), ident[:])
             return bank
 
         def quantise(name, words):
-            width = words.shape[1] // PACK
+            width = words.shape[1] // SLOTS
             codes = kept("codes_" + name, [P, width], U32)
             scales = kept("scales_" + name, [P, width], U8)
             nc.vector.quantize_mx(out=codes[:].bitcast(FP8X4), scales=scales[:], in_=words)
-            mx[name] = (codes, scales)
+            quantised[name] = (codes, scales)
 
-        def phi_matmul(c, g, s, first=0, width=PASS):
-            bank = next_bank([P, width], F32)
-            t0 = c * PASS + first
+        def phi_slot(half, slot, first, width=CHUNK):
+            bank = next_bank([P, width])
             for k in range(GRAD_PASSES):
-                if c == 0:
-                    moving_scales = grad_sc_first[:, k, t0 : t0 + width]
+                if first < CHUNK:
+                    moving_scales = grad_sc_first[:, k, :]
                 else:
-                    moving_scales = grad_sc_rest[:, k, t0 - PASS : t0 - PASS + width]
-                if c < 2:
-                    moving = grad[c][:, k, 2 * first : 2 * (first + width)]
+                    moving_scales = grad_sc_rest[:, k, first - CHUNK : first - CHUNK + width]
+                if first < 2 * CHUNK:
+                    moving = grad_early[first // CHUNK][:, k, :]
                 else:
-                    moving = grad_late[:, k, 2 * (t0 - 2 * PASS) : 2 * (t0 - 2 * PASS + width)]
+                    moving = grad_late[:, k, 2 * (first - 2 * CHUNK) : 2 * (first - 2 * CHUNK + width)]
                 nc.tensor.matmul_mx(
                     out=bank[:],
-                    lhsT=proj[g][:, k, 2 * P * s : 2 * P * (s + 1)].bitcast(FP4X4),
-                    lhsT_scale=proj_sc[g][:, k, P * s : P * (s + 1)],
+                    lhsT=proj[half][:, k, 2 * P * slot : 2 * P * (slot + 1)].bitcast(FP4X4),
+                    lhsT_scale=proj_sc[half][:, k, P * slot : P * (slot + 1)],
                     rhs=moving.bitcast(FP4X4),
                     rhs_scale=moving_scales,
                     start=(k == 0),
                     stop=(k == GRAD_PASSES - 1),
                 )
-            if s == 0:
-                phi_slots[c, g, first] = kept("phi_slots%d%d_%d" % (c, g, first), [P, PACK, width], BF16)
+            if slot == 0:
+                phi_slots[half, first] = kept("phi_slots%d_%d" % (half, first), [P, SLOTS, width], BF16)
             nc.vector.scalar_tensor_tensor(
-                out=phi_slots[c, g, first][:, s, :],
+                out=phi_slots[half, first][:, slot, :],
                 in0=bank[:],
-                scalar=mu_cols[:, s // 2, g, s % 2 : s % 2 + 1],
-                in1=miss_t_all[:, t0 : t0 + width],
+                scalar=mu_cols[:, slot // 2, half, slot % 2 : slot % 2 + 1],
+                in1=miss_t_all[:, first : first + width],
                 op0=ALU.subtract,
                 op1=ALU.mult,
             )
 
-        def interleave_phi(c, g, copy, first=0, width=PASS):
-            words = ring.tile([P, width * PACK], BF16, name="phi_words", tag="phi_words", bufs=4, align_bytes=64)
-            copy(
-                out=words[:].rearrange("p (n s) -> p n s", s=PACK),
-                in_=phi_slots[c, g, first][:].rearrange("p s n -> p n s"),
+        def interleave_phi(half, first, copy):
+            source = phi_slots[half, first]
+            words = ring.tile(
+                [P, source.shape[2] * SLOTS],
+                BF16,
+                name="phi_words",
+                tag="phi_words",
+                bufs=PHI_WORD_BUFFERS,
+                align_bytes=64,
             )
-            phi_words[c, g, first] = words
+            copy(out=words[:].rearrange("p (n s) -> p n s", s=SLOTS), in_=source[:].rearrange("p s n -> p n s"))
+            phi_words[half, first] = words
 
-        def quantise_phi(c, g, first=0):
-            quantise("phi%d%d_%d" % (c, g, first), phi_words[c, g, first][:])
+        def quantise_phi(half, first):
+            quantise("phi%d_%d" % (half, first), phi_words[half, first][:])
 
-        def interleave_kinv(k, g, copy):
-            rows = kinv_early[g][:] if k == 0 else kinv_late[:, :, g * PASS : (g + 1) * PASS]
+        def interleave_kinv(k, half, copy):
+            rows = kinv_early[half][:] if k == 0 else kinv_late[:, :, half * PASS : (half + 1) * PASS]
             copy(
-                out=kinv_words[k, g][:].rearrange("p (s c i j) -> p c s i j", s=PACK, i=4, j=PACK),
-                in_=rows.rearrange("p j (c s i) -> p c s i j", s=PACK, i=4),
+                out=kinv_words[k, half][:].rearrange("p (s c i j) -> p c s i j", s=SLOTS, i=RUN, j=SLOTS),
+                in_=rows.rearrange("p j (c s i) -> p c s i j", s=SLOTS, i=RUN),
             )
 
-        def quantise_kinv(k, g):
-            quantise("kinv%d%d" % (k, g), kinv_words[k, g][:])
+        def quantise_kinv(k, half):
+            quantise("kinv%d%d" % (k, half), kinv_words[k, half][:])
+
+        def sort_query_pairs(pair):
+            source = query_raw[:, pair * 2 * D : (pair + 1) * 2 * D]
+            nc.scalar.copy(
+                out=query_sorted[pair][:].bitcast(F32).rearrange("p (b u w) -> p b u w", u=2, w=P),
+                in_=source.bitcast(F32).rearrange("p (b w u) -> p b u w", u=2, w=P),
+            )
 
         def transpose_queries(a):
-            bank = next_bank([P, FEAT_PASSES, 2, P], F32)
-            words = query_raw[:].bitcast(F32)
+            bank = next_bank([P, HALVES, 2, P])
+            pairs = query_sorted[a // 2][:].bitcast(F32)
             for k in halves:
                 for u in range(2):
-                    first = a * D // 2 + k * PASS // 2
-                    nc.tensor.transpose(bank[:, k, u, :], words[:, first + u : first + PASS // 2 : 2], ident[:])
-            nc.scalar.copy(
-                out=query_words[:].bitcast(F32).rearrange("p (k a n u) -> p a k n u", k=FEAT_PASSES, a=PACK, u=2)[:, a],
-                in_=bank[:].rearrange("p k u n -> p k n u"),
-            )
+                    first = a % 2 * D // 2 + k * PASS // 2 + u * P
+                    nc.tensor.transpose(bank[:, k, u, :], pairs[:, first : first + P], ident[:])
+            by_tile = query_words[:].bitcast(F32).rearrange("p (k a n u) -> p a k n u", k=HALVES, a=QUERY_TILES, u=2)
+            nc.scalar.copy(out=by_tile[:, a], in_=bank[:].rearrange("p k u n -> p k n u"))
 
         def quantise_queries(k):
-            quantise("query%d" % k, query_words[:, k * Q * PACK : (k + 1) * Q * PACK])
+            quantise("query%d" % k, query_words[:, k * Q * SLOTS : (k + 1) * Q * SLOTS])
 
-        def h_matmul(g, a):
-            bank = next_bank([P, PACK, P], F32)
-            for s in range(PACK):
+        def h_tile(half, a):
+            bank = next_bank([P, SLOTS, P])
+            for slot in range(SLOTS):
                 for k in halves:
-                    w_codes, w_scales = mx["kinv%d%d" % (k, g)]
-                    x_codes, x_scales = mx["query%d" % k]
+                    kinv_codes, kinv_scales = quantised["kinv%d%d" % (k, half)]
+                    query_codes, query_scales = quantised["query%d" % k]
                     nc.tensor.matmul_mx(
-                        out=bank[:, s, :],
-                        lhsT=w_codes[:, P * s : P * (s + 1)].bitcast(FP8X4),
-                        lhsT_scale=w_scales[:, P * s : P * (s + 1)],
-                        rhs=x_codes[:, P * a : P * (a + 1)].bitcast(FP8X4),
-                        rhs_scale=x_scales[:, P * a : P * (a + 1)],
+                        out=bank[:, slot, :],
+                        lhsT=kinv_codes[:, P * slot : P * (slot + 1)].bitcast(FP8X4),
+                        lhsT_scale=kinv_scales[:, P * slot : P * (slot + 1)],
+                        rhs=query_codes[:, P * a : P * (a + 1)].bitcast(FP8X4),
+                        rhs_scale=query_scales[:, P * a : P * (a + 1)],
                         start=(k == 0),
-                        stop=(k == FEAT_PASSES - 1),
+                        stop=(k == HALVES - 1),
                     )
             factor = miss_q_all[:].rearrange("p (u n e) -> p u n e", u=2, e=2)[:, a // 2, :, a % 2 : a % 2 + 1]
             nc.vector.tensor_tensor(
-                out=h_words[g][:, a * PASS : (a + 1) * PASS].rearrange("p (n s) -> p n s", s=PACK),
+                out=h_words[half][:, a * PASS : (a + 1) * PASS].rearrange("p (n s) -> p n s", s=SLOTS),
                 in0=bank[:].rearrange("p s n -> p n s"),
-                in1=factor.to_broadcast([P, P, PACK]),
+                in1=factor.to_broadcast([P, P, SLOTS]),
                 op=ALU.mult,
             )
 
-        def quantise_h(g):
-            quantise("h%d" % g, h_words[g][:])
+        def quantise_h(half):
+            quantise("h%d" % half, h_words[half][:])
 
-        def score_pass(c, a, g, first=0, width=PASS):
-            if g == 0:
-                out_banks[c, a, first] = next_bank([P, width], F32)
-            w_codes, w_scales = mx["h%d" % g]
-            if (c, g, first) in phi_words and phi_words[c, g, first].shape[1] == width * PACK:
-                x_codes, x_scales = mx["phi%d%d_%d" % (c, g, first)]
-                columns = slice(0, width)
-            else:
-                x_codes, x_scales = mx["phi%d%d_0" % (c, g)]
-                columns = slice(first, first + width)
-            nc.tensor.matmul_mx(
-                out=out_banks[c, a, first][:],
-                lhsT=w_codes[:, P * a : P * (a + 1)].bitcast(FP8X4),
-                lhsT_scale=w_scales[:, P * a : P * (a + 1)],
-                rhs=x_codes[:, columns].bitcast(FP8X4),
-                rhs_scale=x_scales[:, columns],
-                start=(g == 0),
-                stop=(g == FEAT_PASSES - 1),
-            )
+        def score_bank(a, first, width):
+            bank = next_bank([P, width])
+            for half in halves:
+                h_codes, h_scales = quantised["h%d" % half]
+                start = first if (half, first) in phi_words else first - first % CHUNK
+                phi_codes, phi_scales = quantised["phi%d_%d" % (half, start)]
+                columns = slice(first - start, first - start + width)
+                nc.tensor.matmul_mx(
+                    out=bank[:],
+                    lhsT=h_codes[:, P * a : P * (a + 1)].bitcast(FP8X4),
+                    lhsT_scale=h_scales[:, P * a : P * (a + 1)],
+                    rhs=phi_codes[:, columns].bitcast(FP8X4),
+                    rhs_scale=phi_scales[:, columns],
+                    start=(half == 0),
+                    stop=(half == HALVES - 1),
+                )
+            return bank
 
-        def store_scores(c, a, copy, first=0, width=PASS):
-            scores = ring.tile([P, width], F32, name="scores", tag="scores", bufs=14)
-            copy(out=scores[:], in_=out_banks[c, a, first][:])
-            t0 = c * PASS + first
-            nc.sync.dma_start(out=out.rearrange("(p a) t -> p a t", a=PACK)[:, a, t0 : t0 + width], in_=scores[:])
+        out_tiles = out.rearrange("(p a) t -> p a t", a=QUERY_TILES)
 
-        def scores_of(c, tiles, copy):
-            for a in tiles:
-                for g in halves:
-                    score_pass(c, a, g)
-                store_scores(c, a, copy)
+        def scores(a, first, copy, width=CHUNK):
+            bank = score_bank(a, first, width)
+            result = ring.tile([P, width], F32, name="scores", tag="scores", bufs=SCORE_BUFFERS)
+            copy(out=result[:], in_=bank[:])
+            nc.sync.dma_start(out=out_tiles[:, a, first : first + width], in_=result[:])
 
-        on_s = nc.scalar.copy
-        on_v = nc.vector.tensor_copy
+        def score_pair(a, first, copies, width):
+            banks = [score_bank(a + j, first, width) for j in range(2)]
+            result = ring.tile([P, 2, width], F32, name="scores", tag="scores", bufs=SCORE_BUFFERS)
+            for j in range(2):
+                copies[j](out=result[:, j, :], in_=banks[j][:])
+            nc.sync.dma_start(out=out_tiles[:, a : a + 2, first : first + width], in_=result[:])
 
-        nc.vector.memset(proj_sc_raw[0][:].bitcast(I32), 0)
-        nc.vector.memset(grad_sc_first[:].bitcast(I32), 0)
-        nc.vector.memset(proj_sc_raw[1][:].bitcast(I32), 0)
+        on_scalar = nc.scalar.copy
+        on_vector = nc.vector.tensor_copy
+        chunk0, chunk1, chunk2, chunk3 = range(0, T, CHUNK)
+
         nc.vector.memset(mu_rows[:], 0.0)
+        nc.vector.memset(grad_sc_first[:].bitcast(I32), 0)
+        nc.vector.memset(proj_sc[0][:].bitcast(I32), 0)
+        nc.vector.memset(proj_sc_raw[1][:].bitcast(I32), 0)
         nc.vector.memset(grad_sc_rest[:].bitcast(I32), 0)
         make_identity(nc, ident[:])
+
         nc.scalar.dma_start(out=miss_t_rows[:], in_=miss_t.rearrange("(p e) -> p e", p=P))
-        load_words(proj_raw[0], proj_words, 0, PASS)
-        nc.scalar.dma_start(out=mu_raw[:], in_=mu.rearrange("(g d) -> g d", g=FEAT_PASSES))
+        nc.scalar.dma_start(out=mu_raw[:], in_=mu.rearrange("(g d) -> g d", g=HALVES))
         load_scales(proj_sc_raw[0], proj_scales, 0, PASS)
-        load_words(grad[0], grad_words, 0, PASS)
-        load_scales(grad_sc_first, grad_scales, 0, PASS)
-        load_scales(proj_sc_raw[1], proj_scales, PASS, PASS)
+        load_words(proj_raw[0], proj_words, 0, PASS)
+        load_words(grad_early[0], grad_words, chunk0, CHUNK)
+        load_scales(grad_sc_first, grad_scales, chunk0, CHUNK)
         load_words(proj_raw[1], proj_words, PASS, PASS)
+        load_scales(proj_sc_raw[1], proj_scales, PASS, PASS)
         load_kinv(kinv_early[0], 0, 0, PASS)
-        load_scales(grad_sc_rest, grad_scales, PASS, T - PASS)
-        load_words(grad[1], grad_words, PASS, PASS)
+        load_scales(grad_sc_rest, grad_scales, chunk1, T - CHUNK)
+        load_words(grad_early[1], grad_words, chunk1, CHUNK)
         load_kinv(kinv_early[1], 0, PASS, PASS)
         nc.sync.dma_start(out=miss_q_rows[:], in_=miss_q.rearrange("(p a) -> p a", p=P))
-        nc.sync.dma_start(out=query_raw[:], in_=phi_q.rearrange("(p a) k -> p (a k)", a=PACK))
+        nc.sync.dma_start(out=query_raw[:], in_=phi_q.rearrange("(p a) k -> p (a k)", a=QUERY_TILES))
         load_kinv(kinv_late, 1, 0, D)
-        load_words(grad_late, grad_words, 2 * PASS, 2 * PASS)
+        load_words(grad_late, grad_words, chunk2, T - 2 * CHUNK)
 
+        for quadrant in range(0, P, QUADRANT):
+            sort_proj_scales(0, slice(quadrant, quadrant + SCALE_ROWS))
         sort_proj_words(0)
-        sort_proj_scales(0)
+
         nc.scalar.copy(
-            out=mu_rows[0:FEAT_PASSES, :].rearrange("g (u c i e) -> g u c i e", u=2, i=4, e=2),
-            in_=mu_raw[:].rearrange("g (c u e i) -> g u c i e", u=2, i=4, e=2),
+            out=mu_rows[0:HALVES, :].rearrange("g (u c i e) -> g u c i e", u=2, i=RUN, e=2),
+            in_=mu_raw[:].rearrange("g (c u e i) -> g u c i e", u=2, i=RUN, e=2),
         )
-        miss_t_words = miss_t_all[:].bitcast(F32).rearrange("p (n b u) -> p b n u", b=2, u=4)
+        miss_t_pairs = miss_t_all[:].bitcast(F32).rearrange("p (n b u) -> p b n u", b=2, u=4)
         for b in range(2):
-            spread_bank = spread(miss_t_rows, 4 * b, 4)
-            nc.scalar.copy(out=miss_t_words[:, b], in_=spread_bank[:].rearrange("p u n -> p n u"))
-        mu_bank = next_bank([P, 2, P], F32)
+            miss_t_bank = spread(miss_t_rows, 4 * b, 4)
+            nc.scalar.copy(out=miss_t_pairs[:, b], in_=miss_t_bank[:].rearrange("p u n -> p n u"))
+        mu_bank = next_bank([P, 2, P])
         for u in range(2):
             nc.tensor.transpose(mu_bank[:, u, :], mu_rows[:].bitcast(F32)[:, u * P : (u + 1) * P], ident[:])
-        nc.scalar.copy(
-            out=mu_cols[:].rearrange("p u g e -> p u (g e)").bitcast(F32), in_=mu_bank[:, :, 0:FEAT_PASSES]
-        )
+        nc.scalar.copy(out=mu_cols[:].rearrange("p u g e -> p u (g e)").bitcast(F32), in_=mu_bank[:, :, 0:HALVES])
 
-        interleave_kinv(0, 0, on_s)
-        sort_proj_scales(1)
+        interleave_kinv(0, 0, on_scalar)
         sort_proj_words(1)
-        phi_matmul(0, 0, 0)
-        phi_matmul(0, 0, 1)
-        phi_matmul(0, 0, 2)
-        phi_matmul(0, 0, 3)
-        interleave_phi(0, 0, on_s)
-        phi_matmul(0, 1, 0)
+        phi_slot(0, 0, chunk0)
+        sort_proj_scales(1, slice(0, P))
+        for slot in range(1, SLOTS):
+            phi_slot(0, slot, chunk0)
+        interleave_phi(0, chunk0, on_scalar)
+
+        phi_slot(1, 0, chunk0)
         quantise_kinv(0, 0)
-        phi_matmul(0, 1, 1)
-        phi_matmul(0, 1, 2)
-        phi_matmul(0, 1, 3)
-        interleave_kinv(0, 1, on_v)
-        quantise_phi(0, 0)
-        interleave_phi(0, 1, on_s)
-        phi_matmul(1, 0, 0)
-        phi_matmul(1, 0, 1)
-        phi_matmul(1, 0, 2)
+        for slot in range(1, SLOTS):
+            phi_slot(1, slot, chunk0)
+        interleave_kinv(0, 1, on_vector)
+        quantise_phi(0, chunk0)
+        for pair in range(QUERY_TILES // 2):
+            sort_query_pairs(pair)
+        interleave_kinv(1, 0, on_scalar)
+
+        for slot in range(SLOTS - 1):
+            phi_slot(0, slot, chunk1)
         quantise_kinv(0, 1)
-        phi_matmul(1, 0, 3)
-        interleave_kinv(1, 0, on_s)
-        spread_bank = spread(miss_q_rows, 0, 2)
-        nc.scalar.copy(out=miss_q_all[:].bitcast(F32), in_=spread_bank[:].rearrange("p u n -> p (u n)"))
-        transpose_queries(0)
-        transpose_queries(1)
-        quantise_phi(0, 1)
-        phi_matmul(1, 1, 0)
-        phi_matmul(1, 1, 1)
+        phi_slot(0, SLOTS - 1, chunk1)
+
+        phi_slot(1, 0, chunk1)
+        phi_slot(1, 1, chunk1)
         quantise_kinv(1, 0)
-        transpose_queries(2)
-        transpose_queries(3)
-        interleave_kinv(1, 1, on_s)
-        phi_matmul(1, 1, 2)
+        miss_q_bank = spread(miss_q_rows, 0, 2)
+        nc.scalar.copy(out=miss_q_all[:].bitcast(F32), in_=miss_q_bank[:].rearrange("p u n -> p (u n)"))
+        for a in range(QUERY_TILES):
+            transpose_queries(a)
+        interleave_kinv(1, 1, on_scalar)
+        interleave_phi(1, chunk0, on_scalar)
+        phi_slot(1, 2, chunk1)
+        phi_slot(1, 3, chunk1)
         quantise_queries(0)
-        phi_matmul(1, 1, 3)
+
+        phi_slot(0, 0, chunk2)
         quantise_queries(1)
-        phi_matmul(2, 0, 0)
-        phi_matmul(2, 0, 1)
-        phi_matmul(2, 0, 2)
+        phi_slot(0, 1, chunk2)
+        phi_slot(0, 2, chunk2)
         quantise_kinv(1, 1)
-        phi_matmul(2, 0, 3)
-        interleave_phi(1, 0, on_s)
-        interleave_phi(1, 1, on_s)
-        interleave_phi(2, 0, on_s)
-        for a in range(PACK):
-            h_matmul(0, a)
-        h_matmul(1, 0)
+        phi_slot(0, 3, chunk2)
+        interleave_phi(0, chunk1, on_scalar)
+        interleave_phi(1, chunk1, on_scalar)
+        interleave_phi(0, chunk2, on_scalar)
+
+        for a in range(QUERY_TILES):
+            h_tile(0, a)
+        quantise_phi(1, chunk0)
+        h_tile(1, 0)
         quantise_h(0)
-        for a in range(1, PACK):
-            h_matmul(1, a)
-        phi_matmul(2, 1, 0)
+        for a in range(1, QUERY_TILES):
+            h_tile(1, a)
+
+        phi_slot(1, 0, chunk2)
         quantise_h(1)
-        phi_matmul(2, 1, 1)
-        phi_matmul(2, 1, 2)
-        phi_matmul(2, 1, 3)
-        scores_of(0, range(PACK), on_s)
-        quantise_phi(1, 0)
-        quantise_phi(1, 1)
-        interleave_phi(2, 1, on_s)
-        phi_matmul(3, 0, 0)
-        quantise_phi(2, 0)
-        phi_matmul(3, 0, 1)
-        phi_matmul(3, 0, 2)
-        quantise_phi(2, 1)
-        phi_matmul(3, 0, 3)
-        scores_of(1, (0,), on_s)
-        interleave_phi(3, 0, on_s)
-        scores_of(1, (1, 2), on_v)
-        scores_of(1, (3,), on_s)
-        HALF = PASS // 2
-        for s in range(PACK):
-            phi_matmul(3, 1, s, 0, HALF)
-        quantise_phi(3, 0)
-        interleave_phi(3, 1, on_v, 0, HALF)
-        scores_of(2, (0, 1, 2), on_s)
-        quantise_phi(3, 1, 0)
-        for s in range(PACK):
-            phi_matmul(3, 1, s, HALF, HALF)
-        interleave_phi(3, 1, on_v, HALF, HALF)
-        quantise_phi(3, 1, HALF)
-        scores_of(2, (3,), on_s)
-        for a in range(PACK):
-            for g in halves:
-                score_pass(3, a, g, 0, HALF)
-            store_scores(3, a, on_v if a == 2 else on_s, 0, HALF)
-        for a in range(PACK):
-            for g in halves:
-                score_pass(3, a, g, HALF, HALF)
-            store_scores(3, a, on_v if a % 2 == 0 else on_s, HALF, HALF)
+        for slot in range(1, SLOTS):
+            phi_slot(1, slot, chunk2)
+        interleave_phi(1, chunk2, on_scalar)
+
+        phi_slot(0, 0, chunk3)
+        quantise_phi(0, chunk1)
+        phi_slot(0, 1, chunk3)
+        phi_slot(0, 2, chunk3)
+        quantise_phi(1, chunk1)
+        phi_slot(0, 3, chunk3)
+
+        for a in range(QUERY_TILES):
+            scores(a, chunk0, on_scalar)
+        quantise_phi(0, chunk2)
+        quantise_phi(1, chunk2)
+
+        scores(0, chunk1, on_scalar)
+        interleave_phi(0, chunk3, on_scalar)
+        scores(1, chunk1, on_vector)
+        scores(2, chunk1, on_vector)
+        scores(3, chunk1, on_scalar)
+
+        first_piece, last_piece = chunk3, chunk3 + PIECE
+        for slot in range(SLOTS):
+            phi_slot(1, slot, first_piece, PIECE)
+        quantise_phi(0, chunk3)
+        interleave_phi(1, first_piece, on_vector)
+        for a in range(QUERY_TILES - 1):
+            scores(a, chunk2, on_scalar)
+        quantise_phi(1, first_piece)
+
+        for slot in range(SLOTS):
+            phi_slot(1, slot, last_piece, PIECE)
+        interleave_phi(1, last_piece, on_vector)
+        quantise_phi(1, last_piece)
+        scores(QUERY_TILES - 1, chunk2, on_scalar)
+        score_pair(0, first_piece, (on_scalar, on_scalar), PIECE)
+        score_pair(2, first_piece, (on_vector, on_scalar), PIECE)
+        for a in range(QUERY_TILES):
+            scores(a, last_piece, on_vector if a % 2 == 0 else on_scalar, PIECE)

from contextlib import ExitStack

import concourse.mybir as mybir
from concourse.masks import make_identity

Q, T, D, G = 512, 2048, 1024, 1536
FLOPS = 2 * (Q * D * D + T * D * G + Q * T * D)

F32 = mybir.dt.float32
BF16 = mybir.dt.bfloat16
I32 = mybir.dt.int32
U32 = mybir.dt.uint32
U8 = mybir.dt.uint8
FP8X4 = mybir.dt.float8_e4m3fn_x4
FP4X4 = mybir.dt.float4_e2m1fn_x4
ALU = mybir.AluOpType

P = 128
SLOTS = 4
PASS = P * SLOTS
RUN = 4
QUADRANT = 32
SCALE_ROWS = 4
GRAD_PASSES = G // PASS
HALVES = D // PASS
CHUNK = 512
PIECE = CHUNK // 2
QUERY_TILES = Q // P
BANKS = 8
PHI_WORD_BUFFERS = 4
SCORE_BUFFERS = 14


def tile_trak_attribution_scores_s12_kernel(
    tc, phi_q, kinv, miss_q, grad_words, grad_scales, proj_words, proj_scales, mu, miss_t, out
):
    nc = tc.nc
    with ExitStack() as ctx:
        keep = ctx.enter_context(tc.tile_pool(name="keep", bufs=1))
        ring = ctx.enter_context(tc.tile_pool(name="ring", bufs=1))
        psum = ctx.enter_context(tc.psum_pool(name="psum", bufs=1))
        ctx.enter_context(tc.manual_schedule())

        def kept(name, shape, dtype):
            return keep.tile(shape, dtype, name=name, align_bytes=64)

        banks_taken = []

        def next_bank(shape):
            name = "bank%d" % (len(banks_taken) % BANKS)
            banks_taken.append(name)
            return psum.tile(shape, F32, name=name, tag=name)

        halves = range(HALVES)
        ident = kept("ident", [P, P], F32)
        proj_raw = [kept("proj_raw%d" % half, [P, GRAD_PASSES, 2 * PASS], U8) for half in halves]
        proj = [kept("proj%d" % half, [P, GRAD_PASSES, 2 * PASS], U8) for half in halves]
        proj_sc_raw = [kept("proj_sc_raw%d" % half, [P, GRAD_PASSES, PASS], U8) for half in halves]
        proj_sc = [kept("proj_sc%d" % half, [P, GRAD_PASSES, PASS], U8) for half in halves]
        grad_early = [kept("grad%d" % chunk, [P, GRAD_PASSES, 2 * CHUNK], U8) for chunk in range(2)]
        grad_late = kept("grad_late", [P, GRAD_PASSES, 2 * (T - 2 * CHUNK)], U8)
        grad_sc_first = kept("grad_sc_first", [P, GRAD_PASSES, CHUNK], U8)
        grad_sc_rest = kept("grad_sc_rest", [P, GRAD_PASSES, T - CHUNK], U8)
        mu_raw = kept("mu_raw", [HALVES, PASS], BF16)
        mu_rows = kept("mu_rows", [P, PASS], BF16)
        mu_cols = kept("mu_cols", [P, SLOTS // 2, HALVES, 2], BF16)
        miss_t_rows = kept("miss_t_rows", [P, T // P], BF16)
        miss_q_rows = kept("miss_q_rows", [P, QUERY_TILES], BF16)
        miss_t_all = kept("miss_t_all", [P, T], BF16)
        miss_q_all = kept("miss_q_all", [P, Q], BF16)
        query_raw = kept("query_raw", [P, QUERY_TILES * D], BF16)
        query_sorted = [kept("query_sorted%d" % pair, [P, 2 * D], BF16) for pair in range(QUERY_TILES // 2)]
        query_words = kept("query_words", [P, HALVES * Q * SLOTS], BF16)
        kinv_early = [kept("kinv_early%d" % half, [P, SLOTS, PASS], BF16) for half in halves]
        kinv_late = kept("kinv_late", [P, SLOTS, D], BF16)
        h_words = [kept("h_words%d" % half, [P, Q * SLOTS], BF16) for half in halves]
        kinv_words = {}
        for k in halves:
            for half in halves:
                kinv_words[k, half] = kept("kinv_words%d%d" % (k, half), [P, PASS * SLOTS], BF16)
        phi_slots = {}
        phi_words = {}
        quantised = {}

        def load_scales(tile, scales, first, width):
            rows = scales.bitcast(I32)
            for r in range(SCALE_ROWS):
                nc.sync.dma_start(
                    out=tile[:].bitcast(I32)[r:P:QUADRANT, :, :],
                    in_=rows[:, r :: SCALE_ROWS, first // 4 : (first + width) // 4].rearrange("k q n -> q k n"),
                )

        def load_words(tile, words, first, width):
            nc.sync.dma_start(
                out=tile[:].bitcast(I32),
                in_=words.bitcast(I32)[:, :, first // 2 : (first + width) // 2].rearrange("k p n -> p k n"),
            )

        def load_kinv(tile, k, first, width):
            rows = kinv[k * PASS : (k + 1) * PASS, first : first + width]
            nc.sync.dma_start(out=tile[:], in_=rows.rearrange("(p j) n -> p j n", j=SLOTS))

        def sort_proj_words(half):
            nc.vector.tensor_copy(
                out=proj[half][:].bitcast(I32).rearrange("p k (s c w) -> p s k c w", s=SLOTS, w=2),
                in_=proj_raw[half][:].bitcast(I32).rearrange("p k (c s w) -> p s k c w", s=SLOTS, w=2),
            )

        def sort_proj_scales(half, partitions):
            nc.vector.tensor_copy(
                out=proj_sc[half][partitions].bitcast(I32).rearrange("p k (s c) -> p s k c", s=SLOTS),
                in_=proj_sc_raw[half][partitions].bitcast(I32).rearrange("p k (c s) -> p s k c", s=SLOTS),
            )

        def spread(rows, first_pair, count):
            bank = next_bank([P, count, P])
            pairs = rows[:].bitcast(F32)
            for u in range(count):
                column = pairs[:, first_pair + u : first_pair + u + 1]
                nc.tensor.transpose(bank[:, u, :], column.to_broadcast([P, P]), ident[:])
            return bank

        def quantise(name, words):
            width = words.shape[1] // SLOTS
            codes = kept("codes_" + name, [P, width], U32)
            scales = kept("scales_" + name, [P, width], U8)
            nc.vector.quantize_mx(out=codes[:].bitcast(FP8X4), scales=scales[:], in_=words)
            quantised[name] = (codes, scales)

        def phi_slot(half, slot, first, width=CHUNK):
            bank = next_bank([P, width])
            for k in range(GRAD_PASSES):
                if first < CHUNK:
                    moving_scales = grad_sc_first[:, k, :]
                else:
                    moving_scales = grad_sc_rest[:, k, first - CHUNK : first - CHUNK + width]
                if first < 2 * CHUNK:
                    moving = grad_early[first // CHUNK][:, k, :]
                else:
                    moving = grad_late[:, k, 2 * (first - 2 * CHUNK) : 2 * (first - 2 * CHUNK + width)]
                nc.tensor.matmul_mx(
                    out=bank[:],
                    lhsT=proj[half][:, k, 2 * P * slot : 2 * P * (slot + 1)].bitcast(FP4X4),
                    lhsT_scale=proj_sc[half][:, k, P * slot : P * (slot + 1)],
                    rhs=moving.bitcast(FP4X4),
                    rhs_scale=moving_scales,
                    start=(k == 0),
                    stop=(k == GRAD_PASSES - 1),
                )
            if slot == 0:
                phi_slots[half, first] = kept("phi_slots%d_%d" % (half, first), [P, SLOTS, width], BF16)
            nc.vector.scalar_tensor_tensor(
                out=phi_slots[half, first][:, slot, :],
                in0=bank[:],
                scalar=mu_cols[:, slot // 2, half, slot % 2 : slot % 2 + 1],
                in1=miss_t_all[:, first : first + width],
                op0=ALU.subtract,
                op1=ALU.mult,
            )

        def interleave_phi(half, first, copy):
            source = phi_slots[half, first]
            words = ring.tile(
                [P, source.shape[2] * SLOTS],
                BF16,
                name="phi_words",
                tag="phi_words",
                bufs=PHI_WORD_BUFFERS,
                align_bytes=64,
            )
            copy(out=words[:].rearrange("p (n s) -> p n s", s=SLOTS), in_=source[:].rearrange("p s n -> p n s"))
            phi_words[half, first] = words

        def quantise_phi(half, first):
            quantise("phi%d_%d" % (half, first), phi_words[half, first][:])

        def interleave_kinv(k, half, copy):
            rows = kinv_early[half][:] if k == 0 else kinv_late[:, :, half * PASS : (half + 1) * PASS]
            copy(
                out=kinv_words[k, half][:].rearrange("p (s c i j) -> p c s i j", s=SLOTS, i=RUN, j=SLOTS),
                in_=rows.rearrange("p j (c s i) -> p c s i j", s=SLOTS, i=RUN),
            )

        def quantise_kinv(k, half):
            quantise("kinv%d%d" % (k, half), kinv_words[k, half][:])

        def sort_query_pairs(pair):
            source = query_raw[:, pair * 2 * D : (pair + 1) * 2 * D]
            nc.scalar.copy(
                out=query_sorted[pair][:].bitcast(F32).rearrange("p (b u w) -> p b u w", u=2, w=P),
                in_=source.bitcast(F32).rearrange("p (b w u) -> p b u w", u=2, w=P),
            )

        def transpose_queries(a):
            bank = next_bank([P, HALVES, 2, P])
            pairs = query_sorted[a // 2][:].bitcast(F32)
            for k in halves:
                for u in range(2):
                    first = a % 2 * D // 2 + k * PASS // 2 + u * P
                    nc.tensor.transpose(bank[:, k, u, :], pairs[:, first : first + P], ident[:])
            by_tile = query_words[:].bitcast(F32).rearrange("p (k a n u) -> p a k n u", k=HALVES, a=QUERY_TILES, u=2)
            nc.scalar.copy(out=by_tile[:, a], in_=bank[:].rearrange("p k u n -> p k n u"))

        def quantise_queries(k):
            quantise("query%d" % k, query_words[:, k * Q * SLOTS : (k + 1) * Q * SLOTS])

        def h_tile(half, a):
            bank = next_bank([P, SLOTS, P])
            for slot in range(SLOTS):
                for k in halves:
                    kinv_codes, kinv_scales = quantised["kinv%d%d" % (k, half)]
                    query_codes, query_scales = quantised["query%d" % k]
                    nc.tensor.matmul_mx(
                        out=bank[:, slot, :],
                        lhsT=kinv_codes[:, P * slot : P * (slot + 1)].bitcast(FP8X4),
                        lhsT_scale=kinv_scales[:, P * slot : P * (slot + 1)],
                        rhs=query_codes[:, P * a : P * (a + 1)].bitcast(FP8X4),
                        rhs_scale=query_scales[:, P * a : P * (a + 1)],
                        start=(k == 0),
                        stop=(k == HALVES - 1),
                    )
            factor = miss_q_all[:].rearrange("p (u n e) -> p u n e", u=2, e=2)[:, a // 2, :, a % 2 : a % 2 + 1]
            nc.vector.tensor_tensor(
                out=h_words[half][:, a * PASS : (a + 1) * PASS].rearrange("p (n s) -> p n s", s=SLOTS),
                in0=bank[:].rearrange("p s n -> p n s"),
                in1=factor.to_broadcast([P, P, SLOTS]),
                op=ALU.mult,
            )

        def quantise_h(half):
            quantise("h%d" % half, h_words[half][:])

        def score_bank(a, first, width):
            bank = next_bank([P, width])
            for half in halves:
                h_codes, h_scales = quantised["h%d" % half]
                start = first if (half, first) in phi_words else first - first % CHUNK
                phi_codes, phi_scales = quantised["phi%d_%d" % (half, start)]
                columns = slice(first - start, first - start + width)
                nc.tensor.matmul_mx(
                    out=bank[:],
                    lhsT=h_codes[:, P * a : P * (a + 1)].bitcast(FP8X4),
                    lhsT_scale=h_scales[:, P * a : P * (a + 1)],
                    rhs=phi_codes[:, columns].bitcast(FP8X4),
                    rhs_scale=phi_scales[:, columns],
                    start=(half == 0),
                    stop=(half == HALVES - 1),
                )
            return bank

        out_tiles = out.rearrange("(p a) t -> p a t", a=QUERY_TILES)

        def scores(a, first, copy, width=CHUNK):
            bank = score_bank(a, first, width)
            result = ring.tile([P, width], F32, name="scores", tag="scores", bufs=SCORE_BUFFERS)
            copy(out=result[:], in_=bank[:])
            nc.sync.dma_start(out=out_tiles[:, a, first : first + width], in_=result[:])

        def score_pair(a, first, copies, width):
            banks = [score_bank(a + j, first, width) for j in range(2)]
            result = ring.tile([P, 2, width], F32, name="scores", tag="scores", bufs=SCORE_BUFFERS)
            for j in range(2):
                copies[j](out=result[:, j, :], in_=banks[j][:])
            nc.sync.dma_start(out=out_tiles[:, a : a + 2, first : first + width], in_=result[:])

        on_scalar = nc.scalar.copy
        on_vector = nc.vector.tensor_copy
        chunk0, chunk1, chunk2, chunk3 = range(0, T, CHUNK)

        nc.vector.memset(mu_rows[:], 0.0)
        nc.vector.memset(grad_sc_first[:].bitcast(I32), 0)
        nc.vector.memset(proj_sc[0][:].bitcast(I32), 0)
        nc.vector.memset(proj_sc_raw[1][:].bitcast(I32), 0)
        nc.vector.memset(grad_sc_rest[:].bitcast(I32), 0)
        make_identity(nc, ident[:])

        nc.scalar.dma_start(out=miss_t_rows[:], in_=miss_t.rearrange("(p e) -> p e", p=P))
        nc.scalar.dma_start(out=mu_raw[:], in_=mu.rearrange("(g d) -> g d", g=HALVES))
        load_scales(proj_sc_raw[0], proj_scales, 0, PASS)
        load_words(proj_raw[0], proj_words, 0, PASS)
        load_words(grad_early[0], grad_words, chunk0, CHUNK)
        load_scales(grad_sc_first, grad_scales, chunk0, CHUNK)
        load_words(proj_raw[1], proj_words, PASS, PASS)
        load_scales(proj_sc_raw[1], proj_scales, PASS, PASS)
        load_kinv(kinv_early[0], 0, 0, PASS)
        load_scales(grad_sc_rest, grad_scales, chunk1, T - CHUNK)
        load_words(grad_early[1], grad_words, chunk1, CHUNK)
        load_kinv(kinv_early[1], 0, PASS, PASS)
        nc.sync.dma_start(out=miss_q_rows[:], in_=miss_q.rearrange("(p a) -> p a", p=P))
        nc.sync.dma_start(out=query_raw[:], in_=phi_q.rearrange("(p a) k -> p (a k)", a=QUERY_TILES))
        load_kinv(kinv_late, 1, 0, D)
        load_words(grad_late, grad_words, chunk2, T - 2 * CHUNK)

        for quadrant in range(0, P, QUADRANT):
            sort_proj_scales(0, slice(quadrant, quadrant + SCALE_ROWS))
        sort_proj_words(0)

        nc.scalar.copy(
            out=mu_rows[0:HALVES, :].rearrange("g (u c i e) -> g u c i e", u=2, i=RUN, e=2),
            in_=mu_raw[:].rearrange("g (c u e i) -> g u c i e", u=2, i=RUN, e=2),
        )
        miss_t_pairs = miss_t_all[:].bitcast(F32).rearrange("p (n b u) -> p b n u", b=2, u=4)
        for b in range(2):
            miss_t_bank = spread(miss_t_rows, 4 * b, 4)
            nc.scalar.copy(out=miss_t_pairs[:, b], in_=miss_t_bank[:].rearrange("p u n -> p n u"))
        mu_bank = next_bank([P, 2, P])
        for u in range(2):
            nc.tensor.transpose(mu_bank[:, u, :], mu_rows[:].bitcast(F32)[:, u * P : (u + 1) * P], ident[:])
        nc.scalar.copy(out=mu_cols[:].rearrange("p u g e -> p u (g e)").bitcast(F32), in_=mu_bank[:, :, 0:HALVES])

        interleave_kinv(0, 0, on_scalar)
        sort_proj_words(1)
        phi_slot(0, 0, chunk0)
        sort_proj_scales(1, slice(0, P))
        for slot in range(1, SLOTS):
            phi_slot(0, slot, chunk0)
        interleave_phi(0, chunk0, on_scalar)

        phi_slot(1, 0, chunk0)
        quantise_kinv(0, 0)
        for slot in range(1, SLOTS):
            phi_slot(1, slot, chunk0)
        interleave_kinv(0, 1, on_vector)
        quantise_phi(0, chunk0)
        for pair in range(QUERY_TILES // 2):
            sort_query_pairs(pair)
        interleave_kinv(1, 0, on_scalar)

        for slot in range(SLOTS - 1):
            phi_slot(0, slot, chunk1)
        quantise_kinv(0, 1)
        phi_slot(0, SLOTS - 1, chunk1)

        phi_slot(1, 0, chunk1)
        phi_slot(1, 1, chunk1)
        quantise_kinv(1, 0)
        miss_q_bank = spread(miss_q_rows, 0, 2)
        nc.scalar.copy(out=miss_q_all[:].bitcast(F32), in_=miss_q_bank[:].rearrange("p u n -> p (u n)"))
        for a in range(QUERY_TILES):
            transpose_queries(a)
        interleave_kinv(1, 1, on_scalar)
        interleave_phi(1, chunk0, on_scalar)
        phi_slot(1, 2, chunk1)
        phi_slot(1, 3, chunk1)
        quantise_queries(0)

        phi_slot(0, 0, chunk2)
        quantise_queries(1)
        phi_slot(0, 1, chunk2)
        phi_slot(0, 2, chunk2)
        quantise_kinv(1, 1)
        phi_slot(0, 3, chunk2)
        interleave_phi(0, chunk1, on_scalar)
        interleave_phi(1, chunk1, on_scalar)
        interleave_phi(0, chunk2, on_scalar)

        for a in range(QUERY_TILES):
            h_tile(0, a)
        quantise_phi(1, chunk0)
        h_tile(1, 0)
        quantise_h(0)
        for a in range(1, QUERY_TILES):
            h_tile(1, a)

        phi_slot(1, 0, chunk2)
        quantise_h(1)
        for slot in range(1, SLOTS):
            phi_slot(1, slot, chunk2)
        interleave_phi(1, chunk2, on_scalar)

        phi_slot(0, 0, chunk3)
        quantise_phi(0, chunk1)
        phi_slot(0, 1, chunk3)
        phi_slot(0, 2, chunk3)
        quantise_phi(1, chunk1)
        phi_slot(0, 3, chunk3)

        for a in range(QUERY_TILES):
            scores(a, chunk0, on_scalar)
        quantise_phi(0, chunk2)
        quantise_phi(1, chunk2)

        scores(0, chunk1, on_scalar)
        interleave_phi(0, chunk3, on_scalar)
        scores(1, chunk1, on_vector)
        scores(2, chunk1, on_vector)
        scores(3, chunk1, on_scalar)

        first_piece, last_piece = chunk3, chunk3 + PIECE
        for slot in range(SLOTS):
            phi_slot(1, slot, first_piece, PIECE)
        quantise_phi(0, chunk3)
        interleave_phi(1, first_piece, on_vector)
        for a in range(QUERY_TILES - 1):
            scores(a, chunk2, on_scalar)
        quantise_phi(1, first_piece)

        for slot in range(SLOTS):
            phi_slot(1, slot, last_piece, PIECE)
        interleave_phi(1, last_piece, on_vector)
        quantise_phi(1, last_piece)
        scores(QUERY_TILES - 1, chunk2, on_scalar)
        score_pair(0, first_piece, (on_scalar, on_scalar), PIECE)
        score_pair(2, first_piece, (on_vector, on_scalar), PIECE)
        for a in range(QUERY_TILES):
            scores(a, last_piece, on_vector if a % 2 == 0 else on_scalar, PIECE)
